import numpy as np
import ml_dtypes


def mxq(x, axis, fmt="e4m3"):
    dtype, down = {"e4m3": (ml_dtypes.float8_e4m3fn, 7), "e5m2": (ml_dtypes.float8_e5m2, 14)}[fmt]
    v = np.moveaxis(np.asarray(x, np.float32).astype(ml_dtypes.bfloat16).astype(np.float64), axis, -1)
    blocks = v.reshape(v.shape[:-1] + (-1, 32))
    amax = np.abs(blocks).max(-1, keepdims=True)
    byte = np.maximum(np.where(amax > 0, np.frexp(amax)[1] - 1 + 127, 0) - down, 1)
    scale = np.exp2(byte - 127.0)
    codes = (blocks / scale).astype(np.float32).astype(dtype).astype(np.float64)
    return np.moveaxis((codes * scale).reshape(v.shape), -1, axis)


WIDE = False


def mx_kscale(k):
    if not WIDE:
        return np.ones(k)
    levels = np.array([10, -10, 5, -5, 0])
    if k % 512:
        return np.exp2(np.random.permutation(np.resize(levels, k // 32))).repeat(32)
    a = np.empty((k // 512, 16))
    for p in range(k // 512):
        a[p, :8] = np.random.permutation(np.resize(levels, 8))
        for g in range(8):
            far = levels[np.abs(levels - a[p, g]) >= 10]
            a[p, g + 8] = far[np.random.randint(len(far))]
    return np.exp2(a.ravel()).repeat(32)


def f64(x):
    return np.asarray(x).astype(np.float64)


def striped(idx):
    return np.tile(idx.reshape(-1, 16).T, (8, 1)).astype(np.uint16)


def unstriped(offs):
    return offs[:16].T.reshape(-1).astype(np.int64)


E2M1 = np.array([0.0, 0.5, 1.0, 1.5, 2.0, 3.0, 4.0, 6.0, -0.0, -0.5, -1.0, -1.5, -2.0, -3.0, -4.0, -6.0])


def pack_weight(w, fmt):
    k, n = w.shape
    w = f64(np.asarray(w, np.float32).astype(ml_dtypes.bfloat16)).reshape(k // 32, 32, n)
    amax = np.abs(w).max(1)
    if fmt == "e4m3":
        byte = np.frexp(amax)[1] - 1 + 127 - 7
    else:
        mant, ex = np.frexp(amax / 6.0)
        byte = np.where(mant > 0.5, ex, ex - 1) + 127
    byte = np.clip(np.where(amax > 0, byte, 1), 1, 254)
    scaled = (w * np.exp2(127.0 - byte)[:, None, :]).reshape(k, n).astype(np.float32)
    by_word = np.ascontiguousarray(scaled.reshape(k // 512, 128, 4, n).transpose(0, 1, 3, 2))
    if fmt == "e4m3":
        words = by_word.astype(ml_dtypes.float8_e4m3fn).view(np.uint8)
    else:
        c = by_word.astype(ml_dtypes.float4_e2m1fn).view(np.uint8) & 0xF
        words = (c[..., 0::2] | (c[..., 1::2] << 4)).reshape(k // 512, 128, 2 * n)
    return np.ascontiguousarray(words), np.ascontiguousarray(byte.astype(np.uint8).reshape(k // 512, 16, n))


def unpack_weight(words, scales, fmt):
    g, _, n = scales.shape
    words = np.ascontiguousarray(words).reshape(g, 128, n, -1)
    if fmt == "e4m3":
        vals = words.view(ml_dtypes.float8_e4m3fn).astype(np.float64)
    else:
        nib = np.empty((g, 128, n, 4), np.uint8)
        nib[..., 0::2] = words & 0xF
        nib[..., 1::2] = words >> 4
        vals = E2M1[nib]
    vals = vals * np.repeat(np.exp2(scales.astype(np.float64) - 127.0), 8, axis=1)[..., None]
    return vals.transpose(0, 1, 3, 2).reshape(g * 512, n)


def gelu(v):
    return 0.5 * v * (1.0 + np.tanh(np.sqrt(2.0 / np.pi) * (v + 0.044715 * v**3)))


K, T, S, H, T2, N, P = 1024, 2048, 512, 1024, 1024, 512, 128

def setup_inputs():
    n = np.random.standard_normal
    s = mx_kscale(K)[:, None]
    u = mx_kscale(H)[:, None]
    tab_words, tab_scales = pack_weight(n((K, T)) * s, "e4m3")
    wg_words, wg_scales = pack_weight(1.5 * n((K, H)) / np.sqrt(K) / s, "e2m1")
    return {
        "tab_words": tab_words, "tab_scales": tab_scales,
        "offs": striped(np.random.permutation(T)[:S]),
        "wu": (n((K, H)) / np.sqrt(K) / s * u.T).astype(np.float32),
        "wg_words": wg_words, "wg_scales": wg_scales,
        "offs2": striped(np.random.permutation(T2)[:S]),
        "wgs": np.exp(0.3 * n((P, S))).astype(np.float32),
        "base": (n((H, T2)) * u).astype(np.float32),
        "wd": (n((H, N)) / np.sqrt(H) / u).astype(np.float32),
    }

def reference(tab_words, tab_scales, offs, wu, wg_words, wg_scales, offs2, wgs, base, wd):
    v = unpack_weight(tab_words, tab_scales, "e4m3")[:, unstriped(offs)]
    wg = unpack_weight(wg_words, wg_scales, "e2m1")
    a = mxq(f64(wu), 0, "e4m3").T @ v
    g = wg.T @ v
    h = a * (g / (1.0 + np.exp(-g)))
    page = np.zeros((H, T2))
    page[:, unstriped(offs2)] = np.tile(f64(wgs), (H // P, 1)) * h
    z = page + f64(base)
    zq = mxq(z, 0, "e4m3")
    return mxq(f64(wd), 0, "e4m3").T @ zq

@@ -1,0 +1,295 @@
+from contextlib import ExitStack
+
+import concourse.mybir as mybir
+from concourse.masks import make_identity
+
+K, T, S, H, T2, N = 1024, 2048, 512, 1024, 1024, 512
+FLOPS = 2 * (2 * K * H * S + H * N * T2)
+
+F32 = mybir.dt.float32
+BF16 = mybir.dt.bfloat16
+I32 = mybir.dt.int32
+U32 = mybir.dt.uint32
+U16 = mybir.dt.uint16
+U8 = mybir.dt.uint8
+FP8X4 = mybir.dt.float8_e4m3fn_x4
+FP4X4 = mybir.dt.float4_e2m1fn_x4
+MULT = mybir.AluOpType.mult
+SILU = mybir.ActivationFunctionType.Silu
+
+P = 128
+PACK = 4
+K_PASS = P * PACK
+BANK = 512
+ROW_TILES = H // P
+TILES_PER_PASS = K_PASS // P
+PAGES = 3
+QUARTER = T2 // 4
+WU_CHUNKS = ((0,), (1,), (2, 3), (4, 5), (6, 7))
+WG_FIRST_TILES = 2
+
+
+def tile_list_expert_dispatch_down_kernel(
+    tc, tab_words, tab_scales, offs, wu, wg_words, wg_scales, offs2, wgs, base, wd, out
+):
+    nc = tc.nc
+    with ExitStack() as ctx:
+        lists = ctx.enter_context(tc.tile_pool(name="lists", bufs=1))
+        keep = ctx.enter_context(tc.tile_pool(name="keep", bufs=1))
+        ring = ctx.enter_context(tc.tile_pool(name="ring", bufs=2))
+        psum = ctx.enter_context(tc.psum_pool(name="psum", bufs=1))
+
+        banks = [psum.tile([P, BANK], F32, name=f"bank{b}") for b in range(8)]
+        up_bank, gate_bank, turn_banks = banks[0], banks[1], banks[2:]
+
+        idx = lists.tile([P, S // 16], U16, name="idx")
+        idx2 = lists.tile([P, S // 16], U16, name="idx2")
+        nc.sync.dma_start(idx[:], offs)
+
+        tab_plane = keep.tile([P, 2 * T], U8, name="tab_plane", align_bytes=64)
+        nc.vector.memset(tab_plane[:].bitcast(I32), 0)
+        for q in range(4):
+            nc.scalar.dma_start(
+                tab_plane[32 * q : 32 * q + 4, :].bitcast(I32).rearrange("r (a t) -> r a t", a=2),
+                tab_scales[:, 4 * q : 4 * q + 4, :].bitcast(I32).rearrange("a r t -> r a t"),
+            )
+        wg_plane = keep.tile([P, 2 * H], U8, name="wg_plane", align_bytes=64)
+        nc.gpsimd.memset(wg_plane[:].bitcast(I32), 0)
+        for q in range(4):
+            nc.scalar.dma_start(
+                wg_plane[32 * q : 32 * q + 4, :].bitcast(I32).rearrange("r (a c) -> r a c", a=2),
+                wg_scales[:, 4 * q : 4 * q + 4, :].bitcast(I32).rearrange("a r c -> r a c"),
+            )
+        nc.sync.dma_start(idx2[:], offs2)
+
+        wu_raw = {}
+
+        def load_wu(chunk):
+            width = P * len(chunk)
+            raw = keep.tile([P, 2, PACK, width], F32, name=f"wu_raw{chunk[0]}")
+            for a in range(2):
+                rows = wu[K_PASS * a : K_PASS * (a + 1), P * chunk[0] : P * chunk[0] + width]
+                nc.sync.dma_start(raw[:, a, :, :], rows.rearrange("(p j) c -> p j c", j=PACK))
+            for n, i in enumerate(chunk):
+                wu_raw[i] = raw[:, :, :, P * n : P * (n + 1)]
+
+        wg_codes = {}
+
+        def load_wg(first, last):
+            cols = slice(2 * P * first, 2 * P * last)
+            words = keep.tile([P, 2, 2 * P * (last - first)], U8, name=f"wg_words{first}", align_bytes=64)
+            nc.sync.dma_start(
+                words[:].bitcast(I32), wg_words[:, :, cols].bitcast(I32).rearrange("a p c -> p a c")
+            )
+            for i in range(first, last):
+                wg_codes[i] = words[:, :, 2 * P * (i - first) : 2 * P * (i - first + 1)]
+
+        base_rows = {}
+
+        def load_base(i):
+            rows = keep.tile([P, T2], F32, name=f"base{i}")
+            nc.sync.dma_start(rows[:], base[P * i : P * (i + 1), :])
+            base_rows[i] = rows
+
+        def load_table(a, cuts):
+            words = keep.tile([P, T], I32, name=f"table{a}", align_bytes=64)
+            source = tab_words[a].rearrange("p t i -> p (t i)").bitcast(I32)
+            for left, right in zip(cuts, cuts[1:]):
+                nc.sync.dma_start(words[:, left:right], source[:, left:right])
+            return words
+
+        load_wg(0, WG_FIRST_TILES)
+        table = [load_table(0, (0, 512, 1024, T))]
+        load_wu(WU_CHUNKS[0])
+        table.append(load_table(1, (0, T)))
+        load_wu(WU_CHUNKS[1])
+        weights = keep.tile([P, S], F32, name="weights")
+        nc.sync.dma_start(weights[:], wgs)
+        load_wu(WU_CHUNKS[2])
+        load_wg(WG_FIRST_TILES, ROW_TILES)
+        load_base(0)
+        load_base(1)
+        load_wu(WU_CHUNKS[3])
+        load_base(2)
+        load_base(3)
+        load_wu(WU_CHUNKS[4])
+        wd_raw = []
+        for b in range(2):
+            raw = keep.tile([P, PACK, N], F32, name=f"wd_raw{b}")
+            nc.sync.dma_start(raw[:], wd[K_PASS * b : K_PASS * (b + 1), :].rearrange("(p j) n -> p j n", j=PACK))
+            wd_raw.append(raw)
+        for i in range(4, ROW_TILES):
+            load_base(i)
+
+        pages = [keep.tile([P, T2], F32, name=f"page{n}") for n in range(PAGES)]
+        for page in pages:
+            nc.vector.memset(page[:], 0.0)
+        warm = keep.tile([P, 1], F32, name="warm")
+        nc.scalar.activation(warm[:], pages[0][:, 0:1], SILU)
+        ident = keep.tile([P, P], F32, name="ident")
+        make_identity(nc, ident[:])
+
+        v_codes = [keep.tile([P, S], U32, name=f"v_codes{a}", align_bytes=64) for a in range(2)]
+        v_plane = [keep.tile([P, S], U8, name=f"v_plane{a}", align_bytes=64) for a in range(2)]
+        for a in range(2):
+            nc.vector.tensor_copy(v_plane[a][:], tab_plane[:, T * a : T * (a + 1)].indirect(idx[:]))
+        for a in range(2):
+            nc.vector.tensor_copy(v_codes[a][:], table[a][:].bitcast(U32).indirect(idx[:]))
+
+        wu_codes, wu_plane = {}, {}
+
+        def quantise_wu(i, copy):
+            grouped = keep.tile([P, 2 * P * PACK], BF16, name=f"wu_grouped{i}", tag=f"stage{i}", align_bytes=64)
+            copy(
+                grouped[:].rearrange("p (a c i j) -> p a c j i", a=2, i=4, j=PACK),
+                wu_raw[i].rearrange("p a j (c i) -> p a c j i", i=4),
+            )
+            wu_codes[i] = keep.tile([P, 2 * P], U32, name=f"wu_codes{i}", align_bytes=64)
+            wu_plane[i] = keep.tile([P, 2 * P], U8, name=f"wu_plane{i}", align_bytes=64)
+            nc.vector.quantize_mx(out=wu_codes[i][:].bitcast(FP8X4), scales=wu_plane[i][:], in_=grouped[:])
+
+        def gate_product(i):
+            for a in range(2):
+                nc.tensor.matmul_mx(
+                    out=gate_bank[:],
+                    lhsT=wg_codes[i][:, a, :].bitcast(FP4X4),
+                    lhsT_scale=wg_plane[:, H * a + P * i : H * a + P * (i + 1)],
+                    rhs=v_codes[a][:].bitcast(FP8X4),
+                    rhs_scale=v_plane[a][:],
+                    start=(a == 0),
+                    stop=(a == 1),
+                )
+
+        def up_product(i):
+            for a in range(2):
+                nc.tensor.matmul_mx(
+                    out=up_bank[:],
+                    lhsT=wu_codes[i][:, P * a : P * (a + 1)].bitcast(FP8X4),
+                    lhsT_scale=wu_plane[i][:, P * a : P * (a + 1)],
+                    rhs=v_codes[a][:].bitcast(FP8X4),
+                    rhs_scale=v_plane[a][:],
+                    start=(a == 0),
+                    stop=(a == 1),
+                )
+
+        wd_codes, wd_plane = {}, {}
+
+        def quantise_wd(b, tag):
+            grouped = keep.tile([P, N * PACK], BF16, name=f"wd_grouped{b}", align_bytes=64)
+            nc.scalar.copy(
+                grouped[:].rearrange("p (c i j) -> p c j i", i=4, j=PACK),
+                wd_raw[b][:].rearrange("p j (c i) -> p c j i", i=4),
+            )
+            wd_codes[b] = keep.tile([P, N], U32, name=f"wd_codes{b}", tag=tag, align_bytes=64)
+            wd_plane[b] = keep.tile([P, N], U8, name=f"wd_plane{b}", align_bytes=64)
+            nc.vector.quantize_mx(out=wd_codes[b][:].bitcast(FP8X4), scales=wd_plane[b][:], in_=grouped[:])
+
+        def turn_into(pair, rows, opens):
+            for h in range(2):
+                for c in range(4):
+                    t0 = BANK * h + P * c
+                    nc.tensor.matmul(
+                        pair[h][:, P * c : P * (c + 1)],
+                        lhsT=rows[:, t0 : t0 + P],
+                        rhs=ident[:],
+                        is_transpose=True,
+                        start=(opens and c == 0),
+                        stop=(not opens and c == 3),
+                    )
+
+        z_turned = [
+            [keep.tile([P, 4 * K_PASS], BF16, name=f"z_turned{b}_{h}") for h in range(2)] for b in range(2)
+        ]
+
+        def round_z(i, h, bank, copy):
+            b, part = divmod(i, TILES_PER_PASS)
+            rows = z_turned[b][h][:].rearrange("t (c u p e) -> t c u p e", c=4, u=2, e=2)
+            copy(
+                rows[:, :, :, 32 * part : 32 * (part + 1), :],
+                bank[:].rearrange("t (c p u e) -> t c u p e", c=4, u=2, e=2),
+            )
+
+        z_codes, z_plane = {}, {}
+
+        def quantise_z(b, q, bank, copy):
+            h, m = divmod(q, 2)
+            words = z_turned[b][h][:].bitcast(F32).rearrange("t (c u p) -> t c u p", c=4, u=2)
+            for c in range(2):
+                for u in range(2):
+                    col = P * (2 * c + u)
+                    nc.tensor.transpose(bank[:, col : col + P], words[:, 2 * m + c, u, :], ident[:])
+            grouped = keep.tile([P, 2 * QUARTER], F32, name=f"z_grouped{b}_{q}", align_bytes=64)
+            copy(
+                grouped[:].rearrange("p (c t u) -> p c t u", c=2, u=2),
+                bank[:].rearrange("p (c u t) -> p c t u", c=2, u=2),
+            )
+            z_codes[b, q] = keep.tile([P, QUARTER], U32, name=f"z_codes{b}_{q}", align_bytes=64)
+            z_plane[b, q] = keep.tile([P, QUARTER], U8, name=f"z_plane{b}_{q}", align_bytes=64)
+            nc.vector.quantize_mx(
+                out=z_codes[b, q][:].bitcast(FP8X4), scales=z_plane[b, q][:], in_=grouped[:].bitcast(BF16)
+            )
+
+        def down_pass(pair, b, q):
+            for n in range(4):
+                cols = slice(P * n, P * (n + 1))
+                nc.tensor.matmul_mx(
+                    out=pair[n // 2][:, QUARTER * (n % 2) : QUARTER * (n % 2 + 1)],
+                    lhsT=wd_codes[b][:, cols].bitcast(FP8X4),
+                    lhsT_scale=wd_plane[b][:, cols],
+                    rhs=z_codes[b, q][:].bitcast(FP8X4),
+                    rhs_scale=z_plane[b, q][:],
+                    start=(b == 0 and n % 2 == 0),
+                    stop=(b == 1 and n % 2 == 1),
+                )
+
+        def store(pair, q):
+            for m, copy in enumerate((nc.vector.tensor_copy, nc.scalar.copy)):
+                result = keep.tile([P, 2, QUARTER], F32, name=f"result{q}_{m}")
+                copy(result[:].rearrange("p n t -> p (n t)"), pair[m][:])
+                rows = out[2 * P * m : 2 * P * (m + 1), QUARTER * q : QUARTER * (q + 1)]
+                nc.sync.dma_start(rows.rearrange("(n p) t -> p n t", n=2), result[:])
+
+        on_scalar, on_vector = nc.scalar.copy, nc.vector.tensor_copy
+        spare_pair = turn_banks[4:6]
+
+        quantise_wu(0, on_scalar)
+        gate_product(0)
+        up_product(0)
+        quantise_wu(1, on_vector)
+        last = ROW_TILES - 1
+        for i in range(ROW_TILES):
+            gate = ring.tile([P, S], F32, name="gate")
+            nc.scalar.activation(gate[:], gate_bank[:], SILU)
+            hidden = keep.tile([P, S], F32, name=f"hidden{i}", tag=f"stage{i + 1}", align_bytes=64)
+            nc.vector.tensor_tensor(hidden[:], up_bank[:], gate[:], MULT)
+            if i < last:
+                gate_product(i + 1)
+                up_product(i + 1)
+            pair = turn_banks[2 * (i % 2) : 2 * (i % 2) + 2]
+            turn_into(pair, base_rows[i], True)
+            page = pages[i % PAGES]
+            nc.vector.tensor_tensor(page[:].indirect(idx2[:]), hidden[:], weights[:], MULT)
+            if i + 2 <= last:
+                quantise_wu(i + 2, on_scalar)
+            if i == last:
+                out_pairs = [[up_bank, gate_bank], turn_banks[0:2], spare_pair, pair]
+                down_pass(out_pairs[1], 0, 1)
+                down_pass(out_pairs[0], 0, 0)
+                quantise_wd(1, f"stage{i + 1}")
+            turn_into(pair, page, False)
+            round_z(i, 0, pair[0], on_scalar)
+            round_z(i, 1, pair[1], on_vector if i == last else on_scalar)
+            if i in (4, 5):
+                for m in range(2):
+                    quantise_z(0, 2 * (i - 4) + m, spare_pair[m], on_scalar)
+            if i == 5:
+                quantise_wd(0, "wd_codes0")
+
+        back_banks = spare_pair + pair
+        for q in range(4):
+            quantise_z(1, q, back_banks[q], on_vector if q == 3 else on_scalar)
+        for q in range(4):
+            if q >= 2:
+                down_pass(out_pairs[q], 0, q)
+            down_pass(out_pairs[q], 1, q)
+            store(out_pairs[q], q)

@@ -18,138 +18,136 @@ MULT = mybir.AluOpType.mult
 SILU = mybir.ActivationFunctionType.Silu
 
 P = 128
-PACK = 4
-K_PASS = P * PACK
+SLOTS = 4
+K_PASS = P * SLOTS
+PASSES = 2
+QUADRANT = 32
 BANK = 512
 ROW_TILES = H // P
+LAST = ROW_TILES - 1
 TILES_PER_PASS = K_PASS // P
-PAGES = 3
 QUARTER = T2 // 4
+PAGES = 3
+GATES = 3
+GATE_AHEAD = 2
+WU_AHEAD = 4
 WU_CHUNKS = ((0,), (1,), (2, 3), (4, 5), (6, 7))
 WG_FIRST_TILES = 2
+Z_PARTS = (2, 4)
 
 
 def tile_list_expert_dispatch_down_kernel(
     tc, tab_words, tab_scales, offs, wu, wg_words, wg_scales, offs2, wgs, base, wd, out
 ):
     nc = tc.nc
+    on_scalar, on_vector = nc.scalar.copy, nc.vector.tensor_copy
     with ExitStack() as ctx:
         lists = ctx.enter_context(tc.tile_pool(name="lists", bufs=1))
         keep = ctx.enter_context(tc.tile_pool(name="keep", bufs=1))
-        ring = ctx.enter_context(tc.tile_pool(name="ring", bufs=2))
         psum = ctx.enter_context(tc.psum_pool(name="psum", bufs=1))
 
         banks = [psum.tile([P, BANK], F32, name=f"bank{b}") for b in range(8)]
-        up_bank, gate_bank, turn_banks = banks[0], banks[1], banks[2:]
+        up_bank, gate_bank = banks[0], banks[1]
+        sum_pairs, spare_pair = (banks[2:4], banks[4:6]), banks[6:8]
 
         idx = lists.tile([P, S // 16], U16, name="idx")
         idx2 = lists.tile([P, S // 16], U16, name="idx2")
         nc.sync.dma_start(idx[:], offs)
 
-        tab_plane = keep.tile([P, 2 * T], U8, name="tab_plane", align_bytes=64)
-        nc.vector.memset(tab_plane[:].bitcast(I32), 0)
-        for q in range(4):
-            nc.scalar.dma_start(
-                tab_plane[32 * q : 32 * q + 4, :].bitcast(I32).rearrange("r (a t) -> r a t", a=2),
-                tab_scales[:, 4 * q : 4 * q + 4, :].bitcast(I32).rearrange("a r t -> r a t"),
-            )
-        wg_plane = keep.tile([P, 2 * H], U8, name="wg_plane", align_bytes=64)
-        nc.gpsimd.memset(wg_plane[:].bitcast(I32), 0)
-        for q in range(4):
-            nc.scalar.dma_start(
-                wg_plane[32 * q : 32 * q + 4, :].bitcast(I32).rearrange("r (a c) -> r a c", a=2),
-                wg_scales[:, 4 * q : 4 * q + 4, :].bitcast(I32).rearrange("a r c -> r a c"),
-            )
-        nc.sync.dma_start(idx2[:], offs2)
+        def load_plane(plane, scales):
+            for quad in range(4):
+                live = plane[QUADRANT * quad : QUADRANT * quad + 4, :]
+                nc.scalar.dma_start(
+                    live.bitcast(I32).rearrange("r (a c) -> r a c", a=PASSES),
+                    scales[:, 4 * quad : 4 * quad + 4, :].bitcast(I32).rearrange("a r c -> r a c"),
+                )
 
-        wu_raw = {}
+        tab_plane = keep.tile([P, PASSES * T], U8, name="tab_plane", align_bytes=64)
+        nc.vector.memset(tab_plane[:].bitcast(I32), 0)
+        load_plane(tab_plane, tab_scales)
+        wg_plane = keep.tile([P, PASSES * H], U8, name="wg_plane", align_bytes=64)
+        load_plane(wg_plane, wg_scales)
+
+        warm = keep.tile([P, 2], F32, name="warm")
+        nc.gpsimd.memset(warm[:, 0:1], 0.0)
+        nc.scalar.activation(warm[:, 1:2], warm[:, 0:1], SILU)
+
+        table = [keep.tile([P, T], I32, name=f"table{a}", align_bytes=64) for a in range(PASSES)]
+        wu_raw, wg_codes, base_rows, wd_raw = {}, {}, {}, {}
 
         def load_wu(chunk):
             width = P * len(chunk)
-            raw = keep.tile([P, 2, PACK, width], F32, name=f"wu_raw{chunk[0]}")
-            for a in range(2):
+            raw = keep.tile([P, PASSES, SLOTS, width], F32, name=f"wu_raw{chunk[0]}")
+            for a in range(PASSES):
                 rows = wu[K_PASS * a : K_PASS * (a + 1), P * chunk[0] : P * chunk[0] + width]
-                nc.sync.dma_start(raw[:, a, :, :], rows.rearrange("(p j) c -> p j c", j=PACK))
+                nc.sync.dma_start(raw[:, a, :, :], rows.rearrange("(p j) c -> p j c", j=SLOTS))
             for n, i in enumerate(chunk):
                 wu_raw[i] = raw[:, :, :, P * n : P * (n + 1)]
 
-        wg_codes = {}
-
-        def load_wg(first, last):
-            cols = slice(2 * P * first, 2 * P * last)
-            words = keep.tile([P, 2, 2 * P * (last - first)], U8, name=f"wg_words{first}", align_bytes=64)
-            nc.sync.dma_start(
-                words[:].bitcast(I32), wg_words[:, :, cols].bitcast(I32).rearrange("a p c -> p a c")
-            )
-            for i in range(first, last):
+        def load_wg(first, end):
+            cols = slice(2 * P * first, 2 * P * end)
+            words = keep.tile([P, PASSES, 2 * P * (end - first)], U8, name=f"wg_words{first}", align_bytes=64)
+            for a in range(PASSES):
+                nc.sync.dma_start(words[:, a, :].bitcast(I32), wg_words[a, :, cols].bitcast(I32))
+            for i in range(first, end):
                 wg_codes[i] = words[:, :, 2 * P * (i - first) : 2 * P * (i - first + 1)]
 
-        base_rows = {}
-
         def load_base(i):
-            rows = keep.tile([P, T2], F32, name=f"base{i}")
-            nc.sync.dma_start(rows[:], base[P * i : P * (i + 1), :])
-            base_rows[i] = rows
+            base_rows[i] = keep.tile([P, T2], F32, name=f"base{i}", tag=f"base{i}")
+            nc.sync.dma_start(base_rows[i][:], base[P * i : P * (i + 1), :])
 
-        def load_table(a, cuts):
-            words = keep.tile([P, T], I32, name=f"table{a}", align_bytes=64)
-            source = tab_words[a].rearrange("p t i -> p (t i)").bitcast(I32)
-            for left, right in zip(cuts, cuts[1:]):
-                nc.sync.dma_start(words[:, left:right], source[:, left:right])
-            return words
+        def load_wd(b, tag):
+            wd_raw[b] = keep.tile([P, SLOTS, N], F32, name=f"wd_raw{b}", tag=tag, align_bytes=64)
+            rows = wd[K_PASS * b : K_PASS * (b + 1), :]
+            nc.sync.dma_start(wd_raw[b][:], rows.rearrange("(p j) n -> p j n", j=SLOTS))
 
         load_wg(0, WG_FIRST_TILES)
-        table = [load_table(0, (0, 512, 1024, T))]
+        for a in range(PASSES):
+            nc.sync.dma_start(table[a][:], tab_words[a].rearrange("p t i -> p (t i)").bitcast(I32))
         load_wu(WU_CHUNKS[0])
-        table.append(load_table(1, (0, T)))
+        nc.sync.dma_start(idx2[:], offs2)
         load_wu(WU_CHUNKS[1])
         weights = keep.tile([P, S], F32, name="weights")
         nc.sync.dma_start(weights[:], wgs)
         load_wu(WU_CHUNKS[2])
-        load_wg(WG_FIRST_TILES, ROW_TILES)
         load_base(0)
-        load_base(1)
+        load_wg(WG_FIRST_TILES, ROW_TILES)
         load_wu(WU_CHUNKS[3])
-        load_base(2)
-        load_base(3)
+        load_base(1)
+        load_wd(1, "wd_raw1")
         load_wu(WU_CHUNKS[4])
-        wd_raw = []
-        for b in range(2):
-            raw = keep.tile([P, PACK, N], F32, name=f"wd_raw{b}")
-            nc.sync.dma_start(raw[:], wd[K_PASS * b : K_PASS * (b + 1), :].rearrange("(p j) n -> p j n", j=PACK))
-            wd_raw.append(raw)
-        for i in range(4, ROW_TILES):
+        load_base(2)
+        load_wd(0, f"stage{ROW_TILES}")
+        for i in range(3, ROW_TILES):
             load_base(i)
 
         pages = [keep.tile([P, T2], F32, name=f"page{n}") for n in range(PAGES)]
         for page in pages:
             nc.vector.memset(page[:], 0.0)
-        warm = keep.tile([P, 1], F32, name="warm")
-        nc.scalar.activation(warm[:], pages[0][:, 0:1], SILU)
         ident = keep.tile([P, P], F32, name="ident")
         make_identity(nc, ident[:])
 
-        v_codes = [keep.tile([P, S], U32, name=f"v_codes{a}", align_bytes=64) for a in range(2)]
-        v_plane = [keep.tile([P, S], U8, name=f"v_plane{a}", align_bytes=64) for a in range(2)]
-        for a in range(2):
+        v_plane = [keep.tile([P, S], U8, name=f"v_plane{a}", align_bytes=64) for a in range(PASSES)]
+        for a in range(PASSES):
             nc.vector.tensor_copy(v_plane[a][:], tab_plane[:, T * a : T * (a + 1)].indirect(idx[:]))
-        for a in range(2):
+        v_codes = [keep.tile([P, S], U32, name=f"v_codes{a}", align_bytes=64) for a in range(PASSES)]
+        for a in range(PASSES):
             nc.vector.tensor_copy(v_codes[a][:], table[a][:].bitcast(U32).indirect(idx[:]))
 
-        wu_codes, wu_plane = {}, {}
+        wu_codes, wu_plane, gates = {}, {}, {}
 
         def quantise_wu(i, copy):
-            grouped = keep.tile([P, 2 * P * PACK], BF16, name=f"wu_grouped{i}", tag=f"stage{i}", align_bytes=64)
-            copy(
-                grouped[:].rearrange("p (a c i j) -> p a c j i", a=2, i=4, j=PACK),
-                wu_raw[i].rearrange("p a j (c i) -> p a c j i", i=4),
-            )
-            wu_codes[i] = keep.tile([P, 2 * P], U32, name=f"wu_codes{i}", align_bytes=64)
-            wu_plane[i] = keep.tile([P, 2 * P], U8, name=f"wu_plane{i}", align_bytes=64)
+            grouped = keep.tile([P, PASSES * P * SLOTS], BF16, name=f"wu_grouped{i}", tag=f"stage{i}", align_bytes=64)
+            target = grouped[:].rearrange("p (a c w j) -> p a c j w", a=PASSES, w=4, j=SLOTS)
+            source = wu_raw[i].rearrange("p a j (c w) -> p a c j w", w=4)
+            for passes in (slice(0, 1), slice(1, 2)) if i == 0 else (slice(0, 2),):
+                copy(target[:, passes], source[:, passes])
+            wu_codes[i] = keep.tile([P, PASSES * P], U32, name=f"wu_codes{i}", align_bytes=64)
+            wu_plane[i] = keep.tile([P, PASSES * P], U8, name=f"wu_plane{i}", align_bytes=64)
             nc.vector.quantize_mx(out=wu_codes[i][:].bitcast(FP8X4), scales=wu_plane[i][:], in_=grouped[:])
 
         def gate_product(i):
-            for a in range(2):
+            for a in range(PASSES):
                 nc.tensor.matmul_mx(
                     out=gate_bank[:],
                     lhsT=wg_codes[i][:, a, :].bitcast(FP4X4),
@@ -157,11 +155,11 @@ def tile_list_expert_dispatch_down_kernel(
                     rhs=v_codes[a][:].bitcast(FP8X4),
                     rhs_scale=v_plane[a][:],
                     start=(a == 0),
-                    stop=(a == 1),
+                    stop=(a == PASSES - 1),
                 )
 
         def up_product(i):
-            for a in range(2):
+            for a in range(PASSES):
                 nc.tensor.matmul_mx(
                     out=up_bank[:],
                     lhsT=wu_codes[i][:, P * a : P * (a + 1)].bitcast(FP8X4),
@@ -169,125 +167,164 @@ def tile_list_expert_dispatch_down_kernel(
                     rhs=v_codes[a][:].bitcast(FP8X4),
                     rhs_scale=v_plane[a][:],
                     start=(a == 0),
-                    stop=(a == 1),
+                    stop=(a == PASSES - 1),
                 )
 
-        wd_codes, wd_plane = {}, {}
+        def activate(i):
+            gates[i] = keep.tile([P, S], F32, name=f"gate{i}", tag=f"gate{i % GATES}", align_bytes=64)
+            nc.scalar.activation(gates[i][:], gate_bank[:], SILU)
 
-        def quantise_wd(b, tag):
-            grouped = keep.tile([P, N * PACK], BF16, name=f"wd_grouped{b}", align_bytes=64)
-            nc.scalar.copy(
-                grouped[:].rearrange("p (c i j) -> p c j i", i=4, j=PACK),
-                wd_raw[b][:].rearrange("p j (c i) -> p c j i", i=4),
-            )
-            wd_codes[b] = keep.tile([P, N], U32, name=f"wd_codes{b}", tag=tag, align_bytes=64)
-            wd_plane[b] = keep.tile([P, N], U8, name=f"wd_plane{b}", align_bytes=64)
-            nc.vector.quantize_mx(out=wd_codes[b][:].bitcast(FP8X4), scales=wd_plane[b][:], in_=grouped[:])
-
-        def turn_into(pair, rows, opens):
-            for h in range(2):
-                for c in range(4):
-                    t0 = BANK * h + P * c
+        def turn_into(group, rows, opens):
+            blocks = T2 // P // len(group)
+            for place, bank in enumerate(group):
+                for c in range(blocks):
+                    t0 = P * (blocks * place + c)
                     nc.tensor.matmul(
-                        pair[h][:, P * c : P * (c + 1)],
+                        bank[:, P * c : P * (c + 1)],
                         lhsT=rows[:, t0 : t0 + P],
                         rhs=ident[:],
                         is_transpose=True,
                         start=(opens and c == 0),
-                        stop=(not opens and c == 3),
+                        stop=(not opens and c == blocks - 1),
                     )
 
         z_turned = [
-            [keep.tile([P, 4 * K_PASS], BF16, name=f"z_turned{b}_{h}") for h in range(2)] for b in range(2)
+            [keep.tile([P, T2 * K_PASS // P // parts], BF16, name=f"z_turned{b}_{part}") for part in range(parts)]
+            for b, parts in enumerate(Z_PARTS)
         ]
+        z_grouped, z_codes, z_plane = {}, {}, {}
 
-        def round_z(i, h, bank, copy):
-            b, part = divmod(i, TILES_PER_PASS)
-            rows = z_turned[b][h][:].rearrange("t (c u p e) -> t c u p e", c=4, u=2, e=2)
+        def round_z(i, part, sums, copy):
+            b, quad = divmod(i, TILES_PER_PASS)
+            rows = z_turned[b][part][:].rearrange("t (c u p e) -> t c u p e", u=2, p=P, e=2)
             copy(
-                rows[:, :, :, 32 * part : 32 * (part + 1), :],
-                bank[:].rearrange("t (c p u e) -> t c u p e", c=4, u=2, e=2),
+                rows[:, :, :, QUADRANT * quad : QUADRANT * (quad + 1), :],
+                sums.rearrange("t (c p u e) -> t c u p e", p=QUADRANT, u=2, e=2),
             )
 
-        z_codes, z_plane = {}, {}
-
-        def quantise_z(b, q, bank, copy):
-            h, m = divmod(q, 2)
-            words = z_turned[b][h][:].bitcast(F32).rearrange("t (c u p) -> t c u p", c=4, u=2)
+        def group_z(b, q, bank):
+            part, m = divmod(q, 4 // Z_PARTS[b])
+            words = z_turned[b][part][:].bitcast(F32).rearrange("t (c u p) -> t c u p", p=P, u=2)
             for c in range(2):
                 for u in range(2):
                     col = P * (2 * c + u)
                     nc.tensor.transpose(bank[:, col : col + P], words[:, 2 * m + c, u, :], ident[:])
-            grouped = keep.tile([P, 2 * QUARTER], F32, name=f"z_grouped{b}_{q}", align_bytes=64)
-            copy(
-                grouped[:].rearrange("p (c t u) -> p c t u", c=2, u=2),
+            if m == 0:
+                width = 2 * T2 // Z_PARTS[b]
+                z_grouped[b, part] = keep.tile([P, width], F32, name=f"z_grouped{b}_{part}", align_bytes=64)
+            target = z_grouped[b, part][:, 2 * QUARTER * m : 2 * QUARTER * (m + 1)]
+            on_scalar(
+                target.rearrange("p (c t u) -> p c t u", c=2, u=2),
                 bank[:].rearrange("p (c u t) -> p c t u", c=2, u=2),
             )
-            z_codes[b, q] = keep.tile([P, QUARTER], U32, name=f"z_codes{b}_{q}", align_bytes=64)
-            z_plane[b, q] = keep.tile([P, QUARTER], U8, name=f"z_plane{b}_{q}", align_bytes=64)
-            nc.vector.quantize_mx(
-                out=z_codes[b, q][:].bitcast(FP8X4), scales=z_plane[b, q][:], in_=grouped[:].bitcast(BF16)
+
+        def quantise_z(b, part, plane):
+            width = T2 // Z_PARTS[b]
+            codes = keep.tile([P, width], U32, name=f"z_codes{b}_{part}", align_bytes=64)
+            nc.vector.quantize_mx(out=codes[:].bitcast(FP8X4), scales=plane, in_=z_grouped[b, part][:].bitcast(BF16))
+            for m in range(width // QUARTER):
+                q = part * width // QUARTER + m
+                z_codes[b, q] = codes[:, QUARTER * m : QUARTER * (m + 1)]
+                z_plane[b, q] = plane[:, QUARTER * m : QUARTER * (m + 1)]
+
+        wd_grouped = [keep.tile([P, N * SLOTS], BF16, name=f"wd_grouped{b}", align_bytes=64) for b in range(PASSES)]
+        wd_codes, wd_plane = {}, {}
+
+        def group_wd(b, n):
+            target = wd_grouped[b][:, SLOTS * P * n : SLOTS * P * (n + 1)]
+            on_scalar(
+                target.rearrange("p (c w j) -> p c j w", w=4, j=SLOTS),
+                wd_raw[b][:, :, P * n : P * (n + 1)].rearrange("p j (c w) -> p c j w", w=4),
             )
 
+        def quantise_wd(b, plane):
+            wd_codes[b] = keep.tile([P, N], U32, name=f"wd_codes{b}", align_bytes=64)
+            wd_plane[b] = plane
+            nc.vector.quantize_mx(out=wd_codes[b][:].bitcast(FP8X4), scales=plane, in_=wd_grouped[b][:])
+
         def down_pass(pair, b, q):
-            for n in range(4):
+            for n in range(N // P):
                 cols = slice(P * n, P * (n + 1))
                 nc.tensor.matmul_mx(
                     out=pair[n // 2][:, QUARTER * (n % 2) : QUARTER * (n % 2 + 1)],
                     lhsT=wd_codes[b][:, cols].bitcast(FP8X4),
                     lhsT_scale=wd_plane[b][:, cols],
-                    rhs=z_codes[b, q][:].bitcast(FP8X4),
-                    rhs_scale=z_plane[b, q][:],
+                    rhs=z_codes[b, q].bitcast(FP8X4),
+                    rhs_scale=z_plane[b, q],
                     start=(b == 0 and n % 2 == 0),
-                    stop=(b == 1 and n % 2 == 1),
+                    stop=(b == PASSES - 1 and n % 2 == 1),
                 )
 
         def store(pair, q):
-            for m, copy in enumerate((nc.vector.tensor_copy, nc.scalar.copy)):
-                result = keep.tile([P, 2, QUARTER], F32, name=f"result{q}_{m}")
+            for m, copy in enumerate((on_vector, on_scalar)):
+                result = keep.tile([P, 2, QUARTER], F32, name=f"result{q}_{m}", tag=f"base{2 * q + m}")
                 copy(result[:].rearrange("p n t -> p (n t)"), pair[m][:])
                 rows = out[2 * P * m : 2 * P * (m + 1), QUARTER * q : QUARTER * (q + 1)]
                 nc.sync.dma_start(rows.rearrange("(n p) t -> p n t", n=2), result[:])
 
-        on_scalar, on_vector = nc.scalar.copy, nc.vector.tensor_copy
-        spare_pair = turn_banks[4:6]
+        def new_plane(name, width, tag):
+            return keep.tile([P, width], U8, name=name, tag=tag, align_bytes=64)[:]
 
         quantise_wu(0, on_scalar)
         gate_product(0)
         up_product(0)
+        activate(0)
         quantise_wu(1, on_vector)
-        last = ROW_TILES - 1
+        gate_product(1)
+        activate(1)
+
+        wd_pieces = [(b, n) for b in (1, 0) for n in range(N // P)]
         for i in range(ROW_TILES):
-            gate = ring.tile([P, S], F32, name="gate")
-            nc.scalar.activation(gate[:], gate_bank[:], SILU)
             hidden = keep.tile([P, S], F32, name=f"hidden{i}", tag=f"stage{i + 1}", align_bytes=64)
-            nc.vector.tensor_tensor(hidden[:], up_bank[:], gate[:], MULT)
-            if i < last:
-                gate_product(i + 1)
+            nc.vector.tensor_tensor(hidden[:], up_bank[:], gates[i][:], MULT)
+            if i < LAST:
                 up_product(i + 1)
-            pair = turn_banks[2 * (i % 2) : 2 * (i % 2) + 2]
-            turn_into(pair, base_rows[i], True)
+            if 0 < i <= LAST - WU_AHEAD:
+                quantise_wu(i + WU_AHEAD, on_scalar)
+            if i == LAST:
+                quantise_wd(0, new_plane("wd_plane0", N, "wd_plane0"))
+            if i <= LAST - GATE_AHEAD:
+                gate_product(i + GATE_AHEAD)
+                activate(i + GATE_AHEAD)
+            group = sum_pairs[i % 2] + (spare_pair if i == LAST else [])
+            turn_into(group, base_rows[i], True)
             page = pages[i % PAGES]
             nc.vector.tensor_tensor(page[:].indirect(idx2[:]), hidden[:], weights[:], MULT)
-            if i + 2 <= last:
-                quantise_wu(i + 2, on_scalar)
-            if i == last:
-                out_pairs = [[up_bank, gate_bank], turn_banks[0:2], spare_pair, pair]
-                down_pass(out_pairs[1], 0, 1)
-                down_pass(out_pairs[0], 0, 0)
-                quantise_wd(1, f"stage{i + 1}")
-            turn_into(pair, page, False)
-            round_z(i, 0, pair[0], on_scalar)
-            round_z(i, 1, pair[1], on_vector if i == last else on_scalar)
-            if i in (4, 5):
+            if i == 0:
+                for ahead in range(2, WU_AHEAD + 1):
+                    quantise_wu(ahead, on_scalar)
+            else:
+                for b, n in wd_pieces[:-1][2 * (i - 1) : 2 * i]:
+                    group_wd(b, n)
+            if i == LAST:
+                out_pairs = [[up_bank, gate_bank], sum_pairs[0], group[0:2], group[2:4]]
+                for q in range(2):
+                    down_pass(out_pairs[q], 0, q)
+            turn_into(group, page, False)
+            if i == LAST:
+                late = new_plane("late_planes", 2 * QUARTER + N, f"stage{i + 1}")
+                quantise_wd(1, late[:, 2 * QUARTER :])
+                for q in range(4):
+                    round_z(i, q, group[q][:, :QUARTER], on_scalar if q < 2 else on_vector)
+            else:
+                parts = Z_PARTS[i // TILES_PER_PASS]
+                width = T2 // parts
+                for part in range(parts):
+                    first = width * part % BANK
+                    round_z(i, part, group[width * part // BANK][:, first : first + width], on_scalar)
+            if i in (TILES_PER_PASS, TILES_PER_PASS + 1):
                 for m in range(2):
-                    quantise_z(0, 2 * (i - 4) + m, spare_pair[m], on_scalar)
-            if i == 5:
-                quantise_wd(0, "wd_codes0")
+                    group_z(0, 2 * (i - TILES_PER_PASS) + m, spare_pair[m])
+            if i == TILES_PER_PASS + 1:
+                group_wd(*wd_pieces[-1])
+            if i == LAST - 1:
+                quantise_z(0, 0, new_plane("z_plane0_0", 2 * QUARTER, f"stage{i + 1}"))
 
-        back_banks = spare_pair + pair
         for q in range(4):
-            quantise_z(1, q, back_banks[q], on_vector if q == 3 else on_scalar)
+            group_z(1, q, group[q])
+            quantise_z(1, q, new_plane(f"z_plane1_{q}", QUARTER, f"z_plane1_{q}"))
+            if q == 1:
+                quantise_z(0, 1, late[:, : 2 * QUARTER])
         for q in range(4):
             if q >= 2:
                 down_pass(out_pairs[q], 0, q)

@@ -68,10 +68,6 @@ def tile_list_expert_dispatch_down_kernel(
         wg_plane = keep.tile([P, PASSES * H], U8, name="wg_plane", align_bytes=64)
         load_plane(wg_plane, wg_scales)
 
-        warm = keep.tile([P, 2], F32, name="warm")
-        nc.gpsimd.memset(warm[:, 0:1], 0.0)
-        nc.scalar.activation(warm[:, 1:2], warm[:, 0:1], SILU)
-
         table = [keep.tile([P, T], I32, name=f"table{a}", align_bytes=64) for a in range(PASSES)]
         wu_raw, wg_codes, base_rows, wd_raw = {}, {}, {}, {}
 

@@ -57,16 +57,14 @@ def tile_list_expert_dispatch_down_kernel(
         def load_plane(plane, scales):
             for quad in range(4):
                 live = plane[QUADRANT * quad : QUADRANT * quad + 4, :]
-                nc.scalar.dma_start(
+                nc.sync.dma_start(
                     live.bitcast(I32).rearrange("r (a c) -> r a c", a=PASSES),
                     scales[:, 4 * quad : 4 * quad + 4, :].bitcast(I32).rearrange("a r c -> r a c"),
                 )
 
         tab_plane = keep.tile([P, PASSES * T], U8, name="tab_plane", align_bytes=64)
         nc.vector.memset(tab_plane[:].bitcast(I32), 0)
-        load_plane(tab_plane, tab_scales)
         wg_plane = keep.tile([P, PASSES * H], U8, name="wg_plane", align_bytes=64)
-        load_plane(wg_plane, wg_scales)
 
         table = [keep.tile([P, T], I32, name=f"table{a}", align_bytes=64) for a in range(PASSES)]
         wu_raw, wg_codes, base_rows, wd_raw = {}, {}, {}, {}
@@ -83,8 +81,7 @@ def tile_list_expert_dispatch_down_kernel(
         def load_wg(first, end):
             cols = slice(2 * P * first, 2 * P * end)
             words = keep.tile([P, PASSES, 2 * P * (end - first)], U8, name=f"wg_words{first}", align_bytes=64)
-            for a in range(PASSES):
-                nc.sync.dma_start(words[:, a, :].bitcast(I32), wg_words[a, :, cols].bitcast(I32))
+            nc.sync.dma_start(words[:].bitcast(I32), wg_words[:, :, cols].bitcast(I32).rearrange("a p c -> p a c"))
             for i in range(first, end):
                 wg_codes[i] = words[:, :, 2 * P * (i - first) : 2 * P * (i - first + 1)]
 
@@ -97,14 +94,19 @@ def tile_list_expert_dispatch_down_kernel(
             rows = wd[K_PASS * b : K_PASS * (b + 1), :]
             nc.sync.dma_start(wd_raw[b][:], rows.rearrange("(p j) n -> p j n", j=SLOTS))
 
-        load_wg(0, WG_FIRST_TILES)
-        for a in range(PASSES):
+        def load_table(a):
             nc.sync.dma_start(table[a][:], tab_words[a].rearrange("p t i -> p (t i)").bitcast(I32))
+
+        load_table(0)
+        load_plane(tab_plane, tab_scales)
         load_wu(WU_CHUNKS[0])
+        load_table(1)
+        load_wg(0, WG_FIRST_TILES)
+        load_plane(wg_plane, wg_scales)
         nc.sync.dma_start(idx2[:], offs2)
-        load_wu(WU_CHUNKS[1])
         weights = keep.tile([P, S], F32, name="weights")
         nc.sync.dma_start(weights[:], wgs)
+        load_wu(WU_CHUNKS[1])
         load_wu(WU_CHUNKS[2])
         load_base(0)
         load_wg(WG_FIRST_TILES, ROW_TILES)
@@ -124,11 +126,10 @@ def tile_list_expert_dispatch_down_kernel(
         make_identity(nc, ident[:])
 
         v_plane = [keep.tile([P, S], U8, name=f"v_plane{a}", align_bytes=64) for a in range(PASSES)]
-        for a in range(PASSES):
-            nc.vector.tensor_copy(v_plane[a][:], tab_plane[:, T * a : T * (a + 1)].indirect(idx[:]))
         v_codes = [keep.tile([P, S], U32, name=f"v_codes{a}", align_bytes=64) for a in range(PASSES)]
         for a in range(PASSES):
             nc.vector.tensor_copy(v_codes[a][:], table[a][:].bitcast(U32).indirect(idx[:]))
+            nc.vector.tensor_copy(v_plane[a][:], tab_plane[:, T * a : T * (a + 1)].indirect(idx[:]))
 
         wu_codes, wu_plane, gates = {}, {}, {}
 

@@ -28,11 +28,10 @@ LAST = ROW_TILES - 1
 TILES_PER_PASS = K_PASS // P
 QUARTER = T2 // 4
 PAGES = 3
-GATES = 3
-GATE_AHEAD = 2
-WU_AHEAD = 4
+GATES = 2
+ROUND_LAG = 2
 WU_CHUNKS = ((0,), (1,), (2, 3), (4, 5), (6, 7))
-WG_FIRST_TILES = 2
+WG_CHUNKS = ((0, 2), (2, 4), (4, 8))
 Z_PARTS = (2, 4)
 
 
@@ -48,7 +47,7 @@ def tile_list_expert_dispatch_down_kernel(
 
         banks = [psum.tile([P, BANK], F32, name=f"bank{b}") for b in range(8)]
         up_bank, gate_bank = banks[0], banks[1]
-        sum_pairs, spare_pair = (banks[2:4], banks[4:6]), banks[6:8]
+        sum_pair, late_banks = banks[2:4], banks[4:8]
 
         idx = lists.tile([P, S // 16], U16, name="idx")
         idx2 = lists.tile([P, S // 16], U16, name="idx2")
@@ -71,12 +70,11 @@ def tile_list_expert_dispatch_down_kernel(
 
         def load_wu(chunk):
             width = P * len(chunk)
-            raw = keep.tile([P, PASSES, SLOTS, width], F32, name=f"wu_raw{chunk[0]}")
+            raw = keep.tile([P, PASSES, SLOTS, width], F32, name=f"wu_raw{chunk[0]}", tag=f"wu_raw{chunk[0]}", align_bytes=64)
             for a in range(PASSES):
                 rows = wu[K_PASS * a : K_PASS * (a + 1), P * chunk[0] : P * chunk[0] + width]
                 nc.sync.dma_start(raw[:, a, :, :], rows.rearrange("(p j) c -> p j c", j=SLOTS))
-            for n, i in enumerate(chunk):
-                wu_raw[i] = raw[:, :, :, P * n : P * (n + 1)]
+            wu_raw[chunk] = raw
 
         def load_wg(first, end):
             cols = slice(2 * P * first, 2 * P * end)
@@ -89,86 +87,106 @@ def tile_list_expert_dispatch_down_kernel(
             base_rows[i] = keep.tile([P, T2], F32, name=f"base{i}", tag=f"base{i}")
             nc.sync.dma_start(base_rows[i][:], base[P * i : P * (i + 1), :])
 
-        def load_wd(b, tag):
-            wd_raw[b] = keep.tile([P, SLOTS, N], F32, name=f"wd_raw{b}", tag=tag, align_bytes=64)
+        def load_wd(b):
+            wd_raw[b] = keep.tile([P, SLOTS, N], F32, name=f"wd_raw{b}", tag=f"wd_raw{b}", align_bytes=64)
             rows = wd[K_PASS * b : K_PASS * (b + 1), :]
             nc.sync.dma_start(wd_raw[b][:], rows.rearrange("(p j) n -> p j n", j=SLOTS))
 
         def load_table(a):
             nc.sync.dma_start(table[a][:], tab_words[a].rearrange("p t i -> p (t i)").bitcast(I32))
 
-        load_table(0)
-        load_plane(tab_plane, tab_scales)
         load_wu(WU_CHUNKS[0])
-        load_table(1)
-        load_wg(0, WG_FIRST_TILES)
+        load_plane(tab_plane, tab_scales)
+        load_table(0)
+        load_wg(*WG_CHUNKS[0])
         load_plane(wg_plane, wg_scales)
+        load_table(1)
         nc.sync.dma_start(idx2[:], offs2)
         weights = keep.tile([P, S], F32, name="weights")
         nc.sync.dma_start(weights[:], wgs)
         load_wu(WU_CHUNKS[1])
         load_wu(WU_CHUNKS[2])
-        load_base(0)
-        load_wg(WG_FIRST_TILES, ROW_TILES)
+        load_wg(*WG_CHUNKS[1])
+        load_wd(0)
+        load_wg(*WG_CHUNKS[2])
         load_wu(WU_CHUNKS[3])
+        load_base(0)
         load_base(1)
-        load_wd(1, "wd_raw1")
         load_wu(WU_CHUNKS[4])
         load_base(2)
-        load_wd(0, f"stage{ROW_TILES}")
+        load_wd(1)
         for i in range(3, ROW_TILES):
             load_base(i)
 
         pages = [keep.tile([P, T2], F32, name=f"page{n}") for n in range(PAGES)]
         for page in pages:
-            nc.vector.memset(page[:], 0.0)
+            nc.gpsimd.memset(page[:], 0.0)
         ident = keep.tile([P, P], F32, name="ident")
         make_identity(nc, ident[:])
 
         v_plane = [keep.tile([P, S], U8, name=f"v_plane{a}", align_bytes=64) for a in range(PASSES)]
         v_codes = [keep.tile([P, S], U32, name=f"v_codes{a}", align_bytes=64) for a in range(PASSES)]
         for a in range(PASSES):
-            nc.vector.tensor_copy(v_codes[a][:], table[a][:].bitcast(U32).indirect(idx[:]))
             nc.vector.tensor_copy(v_plane[a][:], tab_plane[:, T * a : T * (a + 1)].indirect(idx[:]))
+        nc.vector.tensor_copy(v_codes[0][:], table[0][:].bitcast(U32).indirect(idx[:]))
 
         wu_codes, wu_plane, gates = {}, {}, {}
 
-        def quantise_wu(i, copy):
-            grouped = keep.tile([P, PASSES * P * SLOTS], BF16, name=f"wu_grouped{i}", tag=f"stage{i}", align_bytes=64)
-            target = grouped[:].rearrange("p (a c w j) -> p a c j w", a=PASSES, w=4, j=SLOTS)
-            source = wu_raw[i].rearrange("p a j (c w) -> p a c j w", w=4)
-            for passes in (slice(0, 1), slice(1, 2)) if i == 0 else (slice(0, 2),):
-                copy(target[:, passes], source[:, passes])
-            wu_codes[i] = keep.tile([P, PASSES * P], U32, name=f"wu_codes{i}", align_bytes=64)
-            wu_plane[i] = keep.tile([P, PASSES * P], U8, name=f"wu_plane{i}", align_bytes=64)
-            nc.vector.quantize_mx(out=wu_codes[i][:].bitcast(FP8X4), scales=wu_plane[i][:], in_=grouped[:])
+        wu_grouped = {}
+
+        def group_wu(chunk):
+            width = P * len(chunk)
+            wu_grouped[chunk] = keep.tile([P, PASSES * width * SLOTS], BF16, name=f"wu_grouped{chunk[0]}", align_bytes=64)
+            target = wu_grouped[chunk][:].rearrange("p (a c w j) -> p a c j w", a=PASSES, w=4, j=SLOTS)
+            source = wu_raw[chunk][:].rearrange("p a j (c w) -> p a c j w", w=4)
+            for a in range(PASSES):
+                on_scalar(target[:, a], source[:, a])
+
+        def quantise_wu(chunk):
+            width = P * len(chunk)
+            codes = keep.tile([P, PASSES * width], U32, name=f"wu_codes{chunk[0]}", align_bytes=64)
+            plane = keep.tile([P, PASSES * width], U8, name=f"wu_plane{chunk[0]}", align_bytes=64)
+            nc.vector.quantize_mx(out=codes[:].bitcast(FP8X4), scales=plane[:], in_=wu_grouped[chunk][:])
+            for n, i in enumerate(chunk):
+                for a in range(PASSES):
+                    cols = slice(width * a + P * n, width * a + P * (n + 1))
+                    wu_codes[i, a], wu_plane[i, a] = codes[:, cols], plane[:, cols]
+
+        def gate_pass(i, a, target, entries, start, stop):
+            nc.tensor.matmul_mx(
+                out=target,
+                lhsT=wg_codes[i][:, a, :].bitcast(FP4X4),
+                lhsT_scale=wg_plane[:, H * a + P * i : H * a + P * (i + 1)],
+                rhs=v_codes[a][:, entries].bitcast(FP8X4),
+                rhs_scale=v_plane[a][:, entries],
+                start=start,
+                stop=stop,
+            )
+
+        def up_pass(i, a, target, entries):
+            nc.tensor.matmul_mx(
+                out=target,
+                lhsT=wu_codes[i, a].bitcast(FP8X4),
+                lhsT_scale=wu_plane[i, a],
+                rhs=v_codes[a][:, entries].bitcast(FP8X4),
+                rhs_scale=v_plane[a][:, entries],
+                start=(a == 0),
+                stop=(a == PASSES - 1),
+            )
 
         def gate_product(i):
             for a in range(PASSES):
-                nc.tensor.matmul_mx(
-                    out=gate_bank[:],
-                    lhsT=wg_codes[i][:, a, :].bitcast(FP4X4),
-                    lhsT_scale=wg_plane[:, H * a + P * i : H * a + P * (i + 1)],
-                    rhs=v_codes[a][:].bitcast(FP8X4),
-                    rhs_scale=v_plane[a][:],
-                    start=(a == 0),
-                    stop=(a == PASSES - 1),
-                )
+                gate_pass(i, a, gate_bank[:], slice(0, S), a == 0, a == PASSES - 1)
 
         def up_product(i):
             for a in range(PASSES):
-                nc.tensor.matmul_mx(
-                    out=up_bank[:],
-                    lhsT=wu_codes[i][:, P * a : P * (a + 1)].bitcast(FP8X4),
-                    lhsT_scale=wu_plane[i][:, P * a : P * (a + 1)],
-                    rhs=v_codes[a][:].bitcast(FP8X4),
-                    rhs_scale=v_plane[a][:],
-                    start=(a == 0),
-                    stop=(a == PASSES - 1),
-                )
+                up_pass(i, a, up_bank[:], slice(0, S))
+
+        def new_gate(i):
+            gates[i] = keep.tile([P, S], F32, name=f"gate{i}", tag=f"gate{i % GATES}", align_bytes=64)
 
         def activate(i):
-            gates[i] = keep.tile([P, S], F32, name=f"gate{i}", tag=f"gate{i % GATES}", align_bytes=64)
+            new_gate(i)
             nc.scalar.activation(gates[i][:], gate_bank[:], SILU)
 
         def turn_into(group, rows, opens):
@@ -227,12 +245,10 @@ def tile_list_expert_dispatch_down_kernel(
         wd_grouped = [keep.tile([P, N * SLOTS], BF16, name=f"wd_grouped{b}", align_bytes=64) for b in range(PASSES)]
         wd_codes, wd_plane = {}, {}
 
-        def group_wd(b, n):
-            target = wd_grouped[b][:, SLOTS * P * n : SLOTS * P * (n + 1)]
-            on_scalar(
-                target.rearrange("p (c w j) -> p c j w", w=4, j=SLOTS),
-                wd_raw[b][:, :, P * n : P * (n + 1)].rearrange("p j (c w) -> p c j w", w=4),
-            )
+        def group_wd(b, h):
+            target = wd_grouped[b][:].rearrange("p (h c w j) -> p h c j w", h=2, w=4, j=SLOTS)
+            source = wd_raw[b][:].rearrange("p j (h c w) -> p h c j w", h=2, w=4)
+            on_scalar(target[:, h], source[:, h])
 
         def quantise_wd(b, plane):
             wd_codes[b] = keep.tile([P, N], U32, name=f"wd_codes{b}", align_bytes=64)
@@ -262,63 +278,95 @@ def tile_list_expert_dispatch_down_kernel(
         def new_plane(name, width, tag):
             return keep.tile([P, width], U8, name=name, tag=tag, align_bytes=64)[:]
 
-        quantise_wu(0, on_scalar)
-        gate_product(0)
-        up_product(0)
-        activate(0)
-        quantise_wu(1, on_vector)
-        gate_product(1)
-        activate(1)
+        def sum_and_round(i):
+            turn_into(sum_pair, base_rows[i], True)
+            turn_into(sum_pair, pages[i % PAGES], False)
+            parts = Z_PARTS[i // TILES_PER_PASS]
+            width = T2 // parts
+            for part in range(parts):
+                first = width * part % BANK
+                round_z(i, part, sum_pair[width * part // BANK][:, first : first + width], on_scalar)
 
-        wd_pieces = [(b, n) for b in (1, 0) for n in range(N // P)]
+        group_wu(WU_CHUNKS[0])
+        quantise_wu(WU_CHUNKS[0])
+        half = S // 2
+        halves = [slice(half * n, half * (n + 1)) for n in range(2)]
+        new_gate(0)
+        for a in range(PASSES):
+            for n, entries in enumerate(halves):
+                if a == PASSES - 1:
+                    places = idx[:, entries.start // 16 : entries.stop // 16]
+                    nc.vector.tensor_copy(v_codes[a][:, entries], table[a][:].bitcast(U32).indirect(places))
+                for m in range(2):
+                    target = late_banks[n][:, P * m : P * (m + 1)]
+                    quarter = slice(entries.start + P * m, entries.start + P * (m + 1))
+                    gate_pass(0, a, target, quarter, a == 0 and m == 0, a == PASSES - 1 and m == 1)
+                up_pass(0, a, late_banks[2 + n][:, :half], entries)
+                if a == PASSES - 1:
+                    nc.scalar.activation(gates[0][:, entries], late_banks[n][:, :half], SILU)
+        gate_product(1)
+
+        def scatter(i, hidden, first, end):
+            places = idx2[:, first // 16 : end // 16]
+            nc.vector.tensor_tensor(pages[i % PAGES][:].indirect(places), hidden, weights[:, first:end], MULT)
+
+        early = keep.tile([P, half], F32, name="hidden_early")
+        nc.vector.tensor_tensor(early[:], late_banks[2][:, :half], gates[0][:, :half], MULT)
+        scatter(0, early[:], 0, half)
+
+        feeds = {0: WU_CHUNKS[1], 1: WU_CHUNKS[2], 2: 0, 3: WU_CHUNKS[3], 4: WU_CHUNKS[4]}
         for i in range(ROW_TILES):
-            hidden = keep.tile([P, S], F32, name=f"hidden{i}", tag=f"stage{i + 1}", align_bytes=64)
-            nc.vector.tensor_tensor(hidden[:], up_bank[:], gates[i][:], MULT)
+            feed = feeds.get(i)
+            if 0 < i < LAST - 1:
+                activate(i)
+                gate_product(i + 1)
+            tag = f"hidden{i}"
+            if feed in WU_CHUNKS:
+                group_wu(feed)
+                tag = f"wu_raw{feed[0]}"
+            elif feed == 0:
+                for h in range(2):
+                    group_wd(0, h)
+                tag = "wd_raw0"
+            first = half if i == 0 else 0
+            hidden = keep.tile([P, S - first], F32, name=f"hidden{i}", tag=tag, align_bytes=64)
+            product = late_banks[3][:, :half] if i == 0 else up_bank[:]
+            nc.vector.tensor_tensor(hidden[:], product, gates[i][:, first:], MULT)
+            if feed in WU_CHUNKS:
+                quantise_wu(feed)
+            elif feed == 0:
+                quantise_wd(0, new_plane("wd_plane0", N, "wd_plane0"))
+            if i == LAST - 1:
+                quantise_z(0, 0, new_plane("z_plane0_0", 2 * QUARTER, "z_plane0_0"))
             if i < LAST:
                 up_product(i + 1)
-            if 0 < i <= LAST - WU_AHEAD:
-                quantise_wu(i + WU_AHEAD, on_scalar)
-            if i == LAST:
-                quantise_wd(0, new_plane("wd_plane0", N, "wd_plane0"))
-            if i <= LAST - GATE_AHEAD:
-                gate_product(i + GATE_AHEAD)
-                activate(i + GATE_AHEAD)
-            group = sum_pairs[i % 2] + (spare_pair if i == LAST else [])
-            turn_into(group, base_rows[i], True)
-            page = pages[i % PAGES]
-            nc.vector.tensor_tensor(page[:].indirect(idx2[:]), hidden[:], weights[:], MULT)
-            if i == 0:
-                for ahead in range(2, WU_AHEAD + 1):
-                    quantise_wu(ahead, on_scalar)
-            else:
-                for b, n in wd_pieces[:-1][2 * (i - 1) : 2 * i]:
-                    group_wd(b, n)
-            if i == LAST:
-                out_pairs = [[up_bank, gate_bank], sum_pairs[0], group[0:2], group[2:4]]
-                for q in range(2):
-                    down_pass(out_pairs[q], 0, q)
-            turn_into(group, page, False)
-            if i == LAST:
-                late = new_plane("late_planes", 2 * QUARTER + N, f"stage{i + 1}")
-                quantise_wd(1, late[:, 2 * QUARTER :])
+            scatter(i, hidden[:], first, S)
+            if i == LAST - 2:
+                group_wd(1, 0)
+                sum_and_round(i - ROUND_LAG)
+                activate(i + 1)
+                gate_product(i + 2)
+                group_wd(1, 1)
                 for q in range(4):
-                    round_z(i, q, group[q][:, :QUARTER], on_scalar if q < 2 else on_vector)
-            else:
-                parts = Z_PARTS[i // TILES_PER_PASS]
-                width = T2 // parts
-                for part in range(parts):
-                    first = width * part % BANK
-                    round_z(i, part, group[width * part // BANK][:, first : first + width], on_scalar)
-            if i in (TILES_PER_PASS, TILES_PER_PASS + 1):
-                for m in range(2):
-                    group_z(0, 2 * (i - TILES_PER_PASS) + m, spare_pair[m])
-            if i == TILES_PER_PASS + 1:
-                group_wd(*wd_pieces[-1])
+                    group_z(0, q, late_banks[q])
+            elif i >= ROUND_LAG:
+                sum_and_round(i - ROUND_LAG)
             if i == LAST - 1:
-                quantise_z(0, 0, new_plane("z_plane0_0", 2 * QUARTER, f"stage{i + 1}"))
+                activate(LAST)
+
+        sum_and_round(LAST - 1)
+        turn_into(late_banks, base_rows[LAST], True)
+        out_pairs = [[up_bank, gate_bank], sum_pair, late_banks[0:2], late_banks[2:4]]
+        for q in range(2):
+            down_pass(out_pairs[q], 0, q)
+        turn_into(late_banks, pages[LAST % PAGES], False)
+        late = new_plane("late_planes", 2 * QUARTER + N, f"hidden{LAST}")
+        quantise_wd(1, late[:, 2 * QUARTER :])
+        for q in range(4):
+            round_z(LAST, q, late_banks[q][:, :QUARTER], on_scalar if q < 2 else on_vector)
 
         for q in range(4):
-            group_z(1, q, group[q])
+            group_z(1, q, late_banks[q])
             quantise_z(1, q, new_plane(f"z_plane1_{q}", QUARTER, f"z_plane1_{q}"))
             if q == 1:
                 quantise_z(0, 1, late[:, : 2 * QUARTER])

@@ -70,11 +70,11 @@ def tile_list_expert_dispatch_down_kernel(
 
         def load_wu(chunk):
             width = P * len(chunk)
-            raw = keep.tile([P, PASSES, SLOTS, width], F32, name=f"wu_raw{chunk[0]}", tag=f"wu_raw{chunk[0]}", align_bytes=64)
             for a in range(PASSES):
+                tag = f"wu_raw{chunk[0]}_{a}"
+                wu_raw[chunk, a] = keep.tile([P, SLOTS, width], F32, name=tag, tag=tag, align_bytes=64)
                 rows = wu[K_PASS * a : K_PASS * (a + 1), P * chunk[0] : P * chunk[0] + width]
-                nc.sync.dma_start(raw[:, a, :, :], rows.rearrange("(p j) c -> p j c", j=SLOTS))
-            wu_raw[chunk] = raw
+                nc.sync.dma_start(wu_raw[chunk, a][:], rows.rearrange("(p j) c -> p j c", j=SLOTS))
 
         def load_wg(first, end):
             cols = slice(2 * P * first, 2 * P * end)
@@ -107,15 +107,16 @@ def tile_list_expert_dispatch_down_kernel(
         load_wu(WU_CHUNKS[1])
         load_wu(WU_CHUNKS[2])
         load_wg(*WG_CHUNKS[1])
-        load_wd(0)
-        load_wg(*WG_CHUNKS[2])
-        load_wu(WU_CHUNKS[3])
         load_base(0)
+        load_wu(WU_CHUNKS[3])
         load_base(1)
-        load_wu(WU_CHUNKS[4])
+        load_wg(*WG_CHUNKS[2])
+        load_wd(0)
         load_base(2)
+        load_wu(WU_CHUNKS[4])
+        load_base(3)
         load_wd(1)
-        for i in range(3, ROW_TILES):
+        for i in range(4, ROW_TILES):
             load_base(i)
 
         pages = [keep.tile([P, T2], F32, name=f"page{n}") for n in range(PAGES)]
@@ -138,9 +139,8 @@ def tile_list_expert_dispatch_down_kernel(
             width = P * len(chunk)
             wu_grouped[chunk] = keep.tile([P, PASSES * width * SLOTS], BF16, name=f"wu_grouped{chunk[0]}", align_bytes=64)
             target = wu_grouped[chunk][:].rearrange("p (a c w j) -> p a c j w", a=PASSES, w=4, j=SLOTS)
-            source = wu_raw[chunk][:].rearrange("p a j (c w) -> p a c j w", w=4)
             for a in range(PASSES):
-                on_scalar(target[:, a], source[:, a])
+                on_scalar(target[:, a], wu_raw[chunk, a][:].rearrange("p j (c w) -> p c j w", w=4))
 
         def quantise_wu(chunk):
             width = P * len(chunk)
@@ -203,15 +203,16 @@ def tile_list_expert_dispatch_down_kernel(
                         stop=(not opens and c == blocks - 1),
                     )
 
-        z_turned = [
-            [keep.tile([P, T2 * K_PASS // P // parts], BF16, name=f"z_turned{b}_{part}") for part in range(parts)]
+        z_turned = {
+            (b, part): keep.tile([P, T2 * K_PASS // P // parts], BF16, name=f"z_turned{b}_{part}")
             for b, parts in enumerate(Z_PARTS)
-        ]
+            for part in range(parts)
+        }
         z_grouped, z_codes, z_plane = {}, {}, {}
 
         def round_z(i, part, sums, copy):
             b, quad = divmod(i, TILES_PER_PASS)
-            rows = z_turned[b][part][:].rearrange("t (c u p e) -> t c u p e", u=2, p=P, e=2)
+            rows = z_turned[b, part][:].rearrange("t (c u p e) -> t c u p e", u=2, p=P, e=2)
             copy(
                 rows[:, :, :, QUADRANT * quad : QUADRANT * (quad + 1), :],
                 sums.rearrange("t (c p u e) -> t c u p e", p=QUADRANT, u=2, e=2),
@@ -219,7 +220,7 @@ def tile_list_expert_dispatch_down_kernel(
 
         def group_z(b, q, bank):
             part, m = divmod(q, 4 // Z_PARTS[b])
-            words = z_turned[b][part][:].bitcast(F32).rearrange("t (c u p) -> t c u p", p=P, u=2)
+            words = z_turned[b, part][:].bitcast(F32).rearrange("t (c u p) -> t c u p", p=P, u=2)
             for c in range(2):
                 for u in range(2):
                     col = P * (2 * c + u)
@@ -314,7 +315,7 @@ def tile_list_expert_dispatch_down_kernel(
         nc.vector.tensor_tensor(early[:], late_banks[2][:, :half], gates[0][:, :half], MULT)
         scatter(0, early[:], 0, half)
 
-        feeds = {0: WU_CHUNKS[1], 1: WU_CHUNKS[2], 2: 0, 3: WU_CHUNKS[3], 4: WU_CHUNKS[4]}
+        feeds = {0: WU_CHUNKS[1], 1: WU_CHUNKS[2], 3: WU_CHUNKS[3], 4: 0, 5: WU_CHUNKS[4]}
         for i in range(ROW_TILES):
             feed = feeds.get(i)
             if 0 < i < LAST - 1:
@@ -323,7 +324,7 @@ def tile_list_expert_dispatch_down_kernel(
             tag = f"hidden{i}"
             if feed in WU_CHUNKS:
                 group_wu(feed)
-                tag = f"wu_raw{feed[0]}"
+                tag = f"wu_raw{feed[0]}_{PASSES - 1}"
             elif feed == 0:
                 for h in range(2):
                     group_wd(0, h)
@@ -342,17 +343,17 @@ def tile_list_expert_dispatch_down_kernel(
                 up_product(i + 1)
             scatter(i, hidden[:], first, S)
             if i == LAST - 2:
-                group_wd(1, 0)
                 sum_and_round(i - ROUND_LAG)
                 activate(i + 1)
                 gate_product(i + 2)
-                group_wd(1, 1)
+                group_wd(1, 0)
                 for q in range(4):
                     group_z(0, q, late_banks[q])
             elif i >= ROUND_LAG:
                 sum_and_round(i - ROUND_LAG)
             if i == LAST - 1:
                 activate(LAST)
+                group_wd(1, 1)
 
         sum_and_round(LAST - 1)
         turn_into(late_banks, base_rows[LAST], True)

@@ -28,8 +28,7 @@ LAST = ROW_TILES - 1
 TILES_PER_PASS = K_PASS // P
 QUARTER = T2 // 4
 PAGES = 3
-GATES = 2
-ROUND_LAG = 2
+GATES = 3
 WU_CHUNKS = ((0,), (1,), (2, 3), (4, 5), (6, 7))
 WG_CHUNKS = ((0, 2), (2, 4), (4, 8))
 Z_PARTS = (2, 4)
@@ -47,7 +46,7 @@ def tile_list_expert_dispatch_down_kernel(
 
         banks = [psum.tile([P, BANK], F32, name=f"bank{b}") for b in range(8)]
         up_bank, gate_bank = banks[0], banks[1]
-        sum_pair, late_banks = banks[2:4], banks[4:8]
+        sum_pairs, spare_pair, late_banks = (banks[2:4], banks[4:6]), banks[6:8], banks[4:8]
 
         idx = lists.tile([P, S // 16], U16, name="idx")
         idx2 = lists.tile([P, S // 16], U16, name="idx2")
@@ -107,16 +106,15 @@ def tile_list_expert_dispatch_down_kernel(
         load_wu(WU_CHUNKS[1])
         load_wu(WU_CHUNKS[2])
         load_wg(*WG_CHUNKS[1])
-        load_base(0)
         load_wu(WU_CHUNKS[3])
-        load_base(1)
+        load_base(0)
         load_wg(*WG_CHUNKS[2])
+        load_wu(WU_CHUNKS[4])
+        load_base(1)
         load_wd(0)
         load_base(2)
-        load_wu(WU_CHUNKS[4])
-        load_base(3)
         load_wd(1)
-        for i in range(4, ROW_TILES):
+        for i in range(3, ROW_TILES):
             load_base(i)
 
         pages = [keep.tile([P, T2], F32, name=f"page{n}") for n in range(PAGES)]
@@ -144,7 +142,7 @@ def tile_list_expert_dispatch_down_kernel(
 
         def quantise_wu(chunk):
             width = P * len(chunk)
-            codes = keep.tile([P, PASSES * width], U32, name=f"wu_codes{chunk[0]}", align_bytes=64)
+            codes = keep.tile([P, PASSES * width], U32, name=f"wu_codes{chunk[0]}", tag="wu_codes", align_bytes=64)
             plane = keep.tile([P, PASSES * width], U8, name=f"wu_plane{chunk[0]}", align_bytes=64)
             nc.vector.quantize_mx(out=codes[:].bitcast(FP8X4), scales=plane[:], in_=wu_grouped[chunk][:])
             for n, i in enumerate(chunk):
@@ -280,6 +278,7 @@ def tile_list_expert_dispatch_down_kernel(
             return keep.tile([P, width], U8, name=name, tag=tag, align_bytes=64)[:]
 
         def sum_and_round(i):
+            sum_pair = sum_pairs[i % 2]
             turn_into(sum_pair, base_rows[i], True)
             turn_into(sum_pair, pages[i % PAGES], False)
             parts = Z_PARTS[i // TILES_PER_PASS]
@@ -315,49 +314,59 @@ def tile_list_expert_dispatch_down_kernel(
         nc.vector.tensor_tensor(early[:], late_banks[2][:, :half], gates[0][:, :half], MULT)
         scatter(0, early[:], 0, half)
 
-        feeds = {0: WU_CHUNKS[1], 1: WU_CHUNKS[2], 3: WU_CHUNKS[3], 4: 0, 5: WU_CHUNKS[4]}
-        for i in range(ROW_TILES):
-            feed = feeds.get(i)
-            if 0 < i < LAST - 1:
-                activate(i)
+        def gate_ahead(i):
+            activate(i)
+            if i < LAST:
                 gate_product(i + 1)
+
+        for i in range(ROW_TILES):
             tag = f"hidden{i}"
-            if feed in WU_CHUNKS:
-                group_wu(feed)
-                tag = f"wu_raw{feed[0]}_{PASSES - 1}"
-            elif feed == 0:
-                for h in range(2):
-                    group_wd(0, h)
-                tag = "wd_raw0"
+            if i <= 1:
+                if i == 1:
+                    gate_ahead(1)
+                group_wu(WU_CHUNKS[i + 1])
+                tag = f"wu_raw{i + 1}_{PASSES - 1}"
             first = half if i == 0 else 0
             hidden = keep.tile([P, S - first], F32, name=f"hidden{i}", tag=tag, align_bytes=64)
             product = late_banks[3][:, :half] if i == 0 else up_bank[:]
             nc.vector.tensor_tensor(hidden[:], product, gates[i][:, first:], MULT)
-            if feed in WU_CHUNKS:
-                quantise_wu(feed)
-            elif feed == 0:
-                quantise_wd(0, new_plane("wd_plane0", N, "wd_plane0"))
-            if i == LAST - 1:
-                quantise_z(0, 0, new_plane("z_plane0_0", 2 * QUARTER, "z_plane0_0"))
+            for chunk in WU_CHUNKS:
+                if chunk[0] == i + 1:
+                    quantise_wu(chunk)
             if i < LAST:
                 up_product(i + 1)
             scatter(i, hidden[:], first, S)
-            if i == LAST - 2:
-                sum_and_round(i - ROUND_LAG)
-                activate(i + 1)
-                gate_product(i + 2)
-                group_wd(1, 0)
+            if 1 <= i <= 4:
+                gate_ahead(i + 1)
+            if i == 1:
+                group_wu(WU_CHUNKS[3])
+            if i == 2:
+                sum_and_round(0)
+                group_wu(WU_CHUNKS[4])
+            if i == 3:
+                sum_and_round(1)
+                for h in range(2):
+                    group_wd(0, h)
+                quantise_wd(0, new_plane("wd_plane0", N, "wd_plane0"))
+            if i == 4:
+                sum_and_round(2)
+                for h in range(2):
+                    group_wd(1, h)
+                gate_ahead(6)
+                sum_and_round(3)
+            if i == 5:
                 for q in range(4):
-                    group_z(0, q, late_banks[q])
-            elif i >= ROUND_LAG:
-                sum_and_round(i - ROUND_LAG)
-            if i == LAST - 1:
-                activate(LAST)
-                group_wd(1, 1)
+                    group_z(0, q, spare_pair[q % 2])
+                    if q == 1:
+                        quantise_z(0, 0, new_plane("z_plane0_0", 2 * QUARTER, "z_plane0_0"))
+                gate_ahead(LAST)
+                sum_and_round(4)
+            if i == 6:
+                sum_and_round(5)
 
         sum_and_round(LAST - 1)
         turn_into(late_banks, base_rows[LAST], True)
-        out_pairs = [[up_bank, gate_bank], sum_pair, late_banks[0:2], late_banks[2:4]]
+        out_pairs = [[up_bank, gate_bank], sum_pairs[0], late_banks[0:2], late_banks[2:4]]
         for q in range(2):
             down_pass(out_pairs[q], 0, q)
         turn_into(late_banks, pages[LAST % PAGES], False)

@@ -119,7 +119,7 @@ def tile_list_expert_dispatch_down_kernel(
 
         pages = [keep.tile([P, T2], F32, name=f"page{n}") for n in range(PAGES)]
         for page in pages:
-            nc.gpsimd.memset(page[:], 0.0)
+            nc.vector.memset(page[:], 0.0)
         ident = keep.tile([P, P], F32, name="ident")
         make_identity(nc, ident[:])
 

@@ -60,9 +60,19 @@ def tile_list_expert_dispatch_down_kernel(
                     scales[:, 4 * quad : 4 * quad + 4, :].bitcast(I32).rearrange("a r c -> r a c"),
                 )
 
+        wg_plane = {}
+
+        def load_wg_plane(first, end):
+            width = P * (end - first)
+            plane = keep.tile([P, PASSES * width], U8, name=f"wg_plane{first}", align_bytes=64)
+            load_plane(plane, wg_scales[:, :, P * first : P * end])
+            for i in range(first, end):
+                for a in range(PASSES):
+                    col = width * a + P * (i - first)
+                    wg_plane[i, a] = plane[:, col : col + P]
+
         tab_plane = keep.tile([P, PASSES * T], U8, name="tab_plane", align_bytes=64)
         nc.vector.memset(tab_plane[:].bitcast(I32), 0)
-        wg_plane = keep.tile([P, PASSES * H], U8, name="wg_plane", align_bytes=64)
 
         table = [keep.tile([P, T], I32, name=f"table{a}", align_bytes=64) for a in range(PASSES)]
         wu_raw, wg_codes, base_rows, wd_raw = {}, {}, {}, {}
@@ -98,7 +108,7 @@ def tile_list_expert_dispatch_down_kernel(
         load_plane(tab_plane, tab_scales)
         load_table(0)
         load_wg(*WG_CHUNKS[0])
-        load_plane(wg_plane, wg_scales)
+        load_wg_plane(*WG_CHUNKS[0])
         load_table(1)
         nc.sync.dma_start(idx2[:], offs2)
         weights = keep.tile([P, S], F32, name="weights")
@@ -106,6 +116,7 @@ def tile_list_expert_dispatch_down_kernel(
         load_wu(WU_CHUNKS[1])
         load_wu(WU_CHUNKS[2])
         load_wg(*WG_CHUNKS[1])
+        load_wg_plane(WG_CHUNKS[1][0], ROW_TILES)
         load_wu(WU_CHUNKS[3])
         load_base(0)
         load_wg(*WG_CHUNKS[2])
@@ -118,10 +129,11 @@ def tile_list_expert_dispatch_down_kernel(
             load_base(i)
 
         pages = [keep.tile([P, T2], F32, name=f"page{n}") for n in range(PAGES)]
+        ident = keep.tile([P, P], F32, name="ident")
+        nc.vector.memset(ident[:], 0.0)
+        make_identity(nc, ident[:], nomemset=True)
         for page in pages:
             nc.vector.memset(page[:], 0.0)
-        ident = keep.tile([P, P], F32, name="ident")
-        make_identity(nc, ident[:])
 
         v_plane = [keep.tile([P, S], U8, name=f"v_plane{a}", align_bytes=64) for a in range(PASSES)]
         v_codes = [keep.tile([P, S], U32, name=f"v_codes{a}", align_bytes=64) for a in range(PASSES)]
@@ -134,27 +146,27 @@ def tile_list_expert_dispatch_down_kernel(
         wu_grouped = {}
 
         def group_wu(chunk):
-            width = P * len(chunk)
-            wu_grouped[chunk] = keep.tile([P, PASSES * width * SLOTS], BF16, name=f"wu_grouped{chunk[0]}", align_bytes=64)
-            target = wu_grouped[chunk][:].rearrange("p (a c w j) -> p a c j w", a=PASSES, w=4, j=SLOTS)
+            tiles = len(chunk)
+            grouped = keep.tile([P, tiles * PASSES * K_PASS], BF16, name=f"wu_grouped{chunk[0]}", align_bytes=64)
+            target = grouped[:].rearrange("p (n a c w j) -> p a n c j w", n=tiles, a=PASSES, w=4, j=SLOTS)
             for a in range(PASSES):
-                on_scalar(target[:, a], wu_raw[chunk, a][:].rearrange("p j (c w) -> p c j w", w=4))
-
-        def quantise_wu(chunk):
-            width = P * len(chunk)
-            codes = keep.tile([P, PASSES * width], U32, name=f"wu_codes{chunk[0]}", tag="wu_codes", align_bytes=64)
-            plane = keep.tile([P, PASSES * width], U8, name=f"wu_plane{chunk[0]}", align_bytes=64)
-            nc.vector.quantize_mx(out=codes[:].bitcast(FP8X4), scales=plane[:], in_=wu_grouped[chunk][:])
+                on_scalar(target[:, a], wu_raw[chunk, a][:].rearrange("p j (n c w) -> p n c j w", n=tiles, w=4))
             for n, i in enumerate(chunk):
-                for a in range(PASSES):
-                    cols = slice(width * a + P * n, width * a + P * (n + 1))
-                    wu_codes[i, a], wu_plane[i, a] = codes[:, cols], plane[:, cols]
+                wu_grouped[i] = grouped[:, PASSES * K_PASS * n : PASSES * K_PASS * (n + 1)]
+
+        def quantise_wu(i):
+            codes = keep.tile([P, PASSES * P], U32, name=f"wu_codes{i}", tag="weight_codes", align_bytes=64)
+            plane = keep.tile([P, PASSES * P], U8, name=f"wu_plane{i}", align_bytes=64)
+            nc.vector.quantize_mx(out=codes[:].bitcast(FP8X4), scales=plane[:], in_=wu_grouped[i])
+            for a in range(PASSES):
+                cols = slice(P * a, P * (a + 1))
+                wu_codes[i, a], wu_plane[i, a] = codes[:, cols], plane[:, cols]
 
         def gate_pass(i, a, target, entries, start, stop):
             nc.tensor.matmul_mx(
                 out=target,
                 lhsT=wg_codes[i][:, a, :].bitcast(FP4X4),
-                lhsT_scale=wg_plane[:, H * a + P * i : H * a + P * (i + 1)],
+                lhsT_scale=wg_plane[i, a],
                 rhs=v_codes[a][:, entries].bitcast(FP8X4),
                 rhs_scale=v_plane[a][:, entries],
                 start=start,
@@ -249,8 +261,8 @@ def tile_list_expert_dispatch_down_kernel(
             source = wd_raw[b][:].rearrange("p j (h c w) -> p h c j w", h=2, w=4)
             on_scalar(target[:, h], source[:, h])
 
-        def quantise_wd(b, plane):
-            wd_codes[b] = keep.tile([P, N], U32, name=f"wd_codes{b}", align_bytes=64)
+        def quantise_wd(b, tag, plane):
+            wd_codes[b] = keep.tile([P, N], U32, name=f"wd_codes{b}", tag=tag, align_bytes=64)
             wd_plane[b] = plane
             nc.vector.quantize_mx(out=wd_codes[b][:].bitcast(FP8X4), scales=plane, in_=wd_grouped[b][:])
 
@@ -288,7 +300,7 @@ def tile_list_expert_dispatch_down_kernel(
                 round_z(i, part, sum_pair[width * part // BANK][:, first : first + width], on_scalar)
 
         group_wu(WU_CHUNKS[0])
-        quantise_wu(WU_CHUNKS[0])
+        quantise_wu(0)
         half = S // 2
         halves = [slice(half * n, half * (n + 1)) for n in range(2)]
         new_gate(0)
@@ -330,11 +342,11 @@ def tile_list_expert_dispatch_down_kernel(
             hidden = keep.tile([P, S - first], F32, name=f"hidden{i}", tag=tag, align_bytes=64)
             product = late_banks[3][:, :half] if i == 0 else up_bank[:]
             nc.vector.tensor_tensor(hidden[:], product, gates[i][:, first:], MULT)
-            for chunk in WU_CHUNKS:
-                if chunk[0] == i + 1:
-                    quantise_wu(chunk)
             if i < LAST:
+                quantise_wu(i + 1)
                 up_product(i + 1)
+            else:
+                quantise_wd(0, "weight_codes", new_plane("wd_plane0", N, "wd_plane0"))
             scatter(i, hidden[:], first, S)
             if 1 <= i <= 4:
                 gate_ahead(i + 1)
@@ -347,7 +359,6 @@ def tile_list_expert_dispatch_down_kernel(
                 sum_and_round(1)
                 for h in range(2):
                     group_wd(0, h)
-                quantise_wd(0, new_plane("wd_plane0", N, "wd_plane0"))
             if i == 4:
                 sum_and_round(2)
                 for h in range(2):
@@ -371,17 +382,22 @@ def tile_list_expert_dispatch_down_kernel(
             down_pass(out_pairs[q], 0, q)
         turn_into(late_banks, pages[LAST % PAGES], False)
         late = new_plane("late_planes", 2 * QUARTER + N, f"hidden{LAST}")
-        quantise_wd(1, late[:, 2 * QUARTER :])
+        quantise_wd(1, "wd_codes1", late[:, 2 * QUARTER :])
         for q in range(4):
             round_z(LAST, q, late_banks[q][:, :QUARTER], on_scalar if q < 2 else on_vector)
+
+        def finish(q):
+            if q >= 2:
+                down_pass(out_pairs[q], 0, q)
+            down_pass(out_pairs[q], 1, q)
+            store(out_pairs[q], q)
 
         for q in range(4):
             group_z(1, q, late_banks[q])
             quantise_z(1, q, new_plane(f"z_plane1_{q}", QUARTER, f"z_plane1_{q}"))
             if q == 1:
                 quantise_z(0, 1, late[:, : 2 * QUARTER])
-        for q in range(4):
-            if q >= 2:
-                down_pass(out_pairs[q], 0, q)
-            down_pass(out_pairs[q], 1, q)
-            store(out_pairs[q], q)
+            if q == 2:
+                finish(0)
+        for q in range(1, 4):
+            finish(q)

@@ -244,14 +244,14 @@ def tile_list_expert_dispatch_down_kernel(
                 bank[:].rearrange("p (c u t) -> p c t u", c=2, u=2),
             )
 
-        def quantise_z(b, part, plane):
-            width = T2 // Z_PARTS[b]
-            codes = keep.tile([P, width], U32, name=f"z_codes{b}_{part}", align_bytes=64)
-            nc.vector.quantize_mx(out=codes[:].bitcast(FP8X4), scales=plane, in_=z_grouped[b, part][:].bitcast(BF16))
-            for m in range(width // QUARTER):
-                q = part * width // QUARTER + m
-                z_codes[b, q] = codes[:, QUARTER * m : QUARTER * (m + 1)]
-                z_plane[b, q] = plane[:, QUARTER * m : QUARTER * (m + 1)]
+        def quantise_z(b, first, end, plane):
+            part, m = divmod(first, 4 // Z_PARTS[b])
+            codes = keep.tile([P, QUARTER * (end - first)], U32, name=f"z_codes{b}_{first}", align_bytes=64)
+            words = z_grouped[b, part][:, 2 * QUARTER * m : 2 * QUARTER * (m + end - first)]
+            nc.vector.quantize_mx(out=codes[:].bitcast(FP8X4), scales=plane, in_=words.bitcast(BF16))
+            for q in range(first, end):
+                cols = slice(QUARTER * (q - first), QUARTER * (q - first + 1))
+                z_codes[b, q], z_plane[b, q] = codes[:, cols], plane[:, cols]
 
         wd_grouped = [keep.tile([P, N * SLOTS], BF16, name=f"wd_grouped{b}", align_bytes=64) for b in range(PASSES)]
         wd_codes, wd_plane = {}, {}
@@ -369,7 +369,7 @@ def tile_list_expert_dispatch_down_kernel(
                 for q in range(4):
                     group_z(0, q, spare_pair[q % 2])
                     if q == 1:
-                        quantise_z(0, 0, new_plane("z_plane0_0", 2 * QUARTER, "z_plane0_0"))
+                        quantise_z(0, 0, 1, new_plane("z_plane0_0", QUARTER, "z_plane0_0"))
                 gate_ahead(LAST)
                 sum_and_round(4)
             if i == 6:
@@ -378,13 +378,14 @@ def tile_list_expert_dispatch_down_kernel(
         sum_and_round(LAST - 1)
         turn_into(late_banks, base_rows[LAST], True)
         out_pairs = [[up_bank, gate_bank], sum_pairs[0], late_banks[0:2], late_banks[2:4]]
-        for q in range(2):
-            down_pass(out_pairs[q], 0, q)
+        down_pass(out_pairs[0], 0, 0)
         turn_into(late_banks, pages[LAST % PAGES], False)
-        late = new_plane("late_planes", 2 * QUARTER + N, f"hidden{LAST}")
-        quantise_wd(1, "wd_codes1", late[:, 2 * QUARTER :])
+        late = new_plane("late_planes", 3 * QUARTER + N, f"hidden{LAST}")
+        quantise_z(0, 1, 2, late[:, 2 * QUARTER : 3 * QUARTER])
+        down_pass(out_pairs[1], 0, 1)
+        quantise_wd(1, "wd_codes1", late[:, 3 * QUARTER :])
         for q in range(4):
-            round_z(LAST, q, late_banks[q][:, :QUARTER], on_scalar if q < 2 else on_vector)
+            round_z(LAST, q, late_banks[q][:, :QUARTER], on_scalar if q < 3 else on_vector)
 
         def finish(q):
             if q >= 2:
@@ -394,9 +395,9 @@ def tile_list_expert_dispatch_down_kernel(
 
         for q in range(4):
             group_z(1, q, late_banks[q])
-            quantise_z(1, q, new_plane(f"z_plane1_{q}", QUARTER, f"z_plane1_{q}"))
+            quantise_z(1, q, q + 1, new_plane(f"z_plane1_{q}", QUARTER, f"z_plane1_{q}"))
             if q == 1:
-                quantise_z(0, 1, late[:, : 2 * QUARTER])
+                quantise_z(0, 2, 4, late[:, : 2 * QUARTER])
             if q == 2:
                 finish(0)
         for q in range(1, 4):

@@ -53,11 +53,11 @@ def tile_list_expert_dispatch_down_kernel(
         nc.sync.dma_start(idx[:], offs)
 
         def load_plane(plane, scales):
-            for quad in range(4):
-                live = plane[QUADRANT * quad : QUADRANT * quad + 4, :]
+            for r in range(4):
+                live = plane[r:P:QUADRANT, :]
                 nc.sync.dma_start(
-                    live.bitcast(I32).rearrange("r (a c) -> r a c", a=PASSES),
-                    scales[:, 4 * quad : 4 * quad + 4, :].bitcast(I32).rearrange("a r c -> r a c"),
+                    live.bitcast(I32).rearrange("q (a c) -> q a c", a=PASSES),
+                    scales[:, r:16:4, :].bitcast(I32).rearrange("a q c -> q a c"),
                 )
 
         wg_plane = {}

@@ -244,9 +244,10 @@ def tile_list_expert_dispatch_down_kernel(
                 bank[:].rearrange("p (c u t) -> p c t u", c=2, u=2),
             )
 
-        def quantise_z(b, first, end, plane):
+        def quantise_z(b, first, end, plane, tag=None):
             part, m = divmod(first, 4 // Z_PARTS[b])
-            codes = keep.tile([P, QUARTER * (end - first)], U32, name=f"z_codes{b}_{first}", align_bytes=64)
+            name = f"z_codes{b}_{first}"
+            codes = keep.tile([P, QUARTER * (end - first)], U32, name=name, tag=tag or name, align_bytes=64)
             words = z_grouped[b, part][:, 2 * QUARTER * m : 2 * QUARTER * (m + end - first)]
             nc.vector.quantize_mx(out=codes[:].bitcast(FP8X4), scales=plane, in_=words.bitcast(BF16))
             for q in range(first, end):
@@ -279,8 +280,10 @@ def tile_list_expert_dispatch_down_kernel(
                     stop=(b == PASSES - 1 and n % 2 == 1),
                 )
 
+        emptied_by = ((on_vector, on_vector), (on_scalar, on_scalar), (on_vector, on_scalar), (on_vector, on_scalar))
+
         def store(pair, q):
-            for m, copy in enumerate((on_vector, on_scalar)):
+            for m, copy in enumerate(emptied_by[q]):
                 result = keep.tile([P, 2, QUARTER], F32, name=f"result{q}_{m}", tag=f"base{2 * q + m}")
                 copy(result[:].rearrange("p n t -> p (n t)"), pair[m][:])
                 rows = out[2 * P * m : 2 * P * (m + 1), QUARTER * q : QUARTER * (q + 1)]
@@ -346,7 +349,7 @@ def tile_list_expert_dispatch_down_kernel(
                 quantise_wu(i + 1)
                 up_product(i + 1)
             else:
-                quantise_wd(0, "weight_codes", new_plane("wd_plane0", N, "wd_plane0"))
+                quantise_z(0, 0, 1, new_plane("z_plane0_0", QUARTER, "z_plane0_0"), "weight_codes")
             scatter(i, hidden[:], first, S)
             if 1 <= i <= 4:
                 gate_ahead(i + 1)
@@ -368,8 +371,6 @@ def tile_list_expert_dispatch_down_kernel(
             if i == 5:
                 for q in range(4):
                     group_z(0, q, spare_pair[q % 2])
-                    if q == 1:
-                        quantise_z(0, 0, 1, new_plane("z_plane0_0", QUARTER, "z_plane0_0"))
                 gate_ahead(LAST)
                 sum_and_round(4)
             if i == 6:
@@ -378,17 +379,17 @@ def tile_list_expert_dispatch_down_kernel(
         sum_and_round(LAST - 1)
         turn_into(late_banks, base_rows[LAST], True)
         out_pairs = [[up_bank, gate_bank], sum_pairs[0], late_banks[0:2], late_banks[2:4]]
-        down_pass(out_pairs[0], 0, 0)
         turn_into(late_banks, pages[LAST % PAGES], False)
-        late = new_plane("late_planes", 3 * QUARTER + N, f"hidden{LAST}")
-        quantise_z(0, 1, 2, late[:, 2 * QUARTER : 3 * QUARTER])
-        down_pass(out_pairs[1], 0, 1)
-        quantise_wd(1, "wd_codes1", late[:, 3 * QUARTER :])
+        late = new_plane("late_planes", 3 * QUARTER + 2 * N, f"hidden{LAST}")
+        quantise_wd(0, "wd_codes0", late[:, 3 * QUARTER + N :])
+        down_pass(out_pairs[0], 0, 0)
+        quantise_wd(1, "wd_codes1", late[:, 3 * QUARTER : 3 * QUARTER + N])
         for q in range(4):
-            round_z(LAST, q, late_banks[q][:, :QUARTER], on_scalar if q < 3 else on_vector)
+            round_z(LAST, q, late_banks[q][:, :QUARTER], on_scalar)
+        quantise_z(0, 1, 2, late[:, 2 * QUARTER : 3 * QUARTER])
 
         def finish(q):
-            if q >= 2:
+            if q >= 1:
                 down_pass(out_pairs[q], 0, q)
             down_pass(out_pairs[q], 1, q)
             store(out_pairs[q], q)

@@ -379,6 +379,8 @@ def tile_list_expert_dispatch_down_kernel(
         sum_and_round(LAST - 1)
         turn_into(late_banks, base_rows[LAST], True)
         out_pairs = [[up_bank, gate_bank], sum_pairs[0], late_banks[0:2], late_banks[2:4]]
+        for n in range(4):
+            gate_pass(LAST, n % PASSES, up_bank[:], slice(0, S), n == 0, n == 3)
         turn_into(late_banks, pages[LAST % PAGES], False)
         late = new_plane("late_planes", 3 * QUARTER + 2 * N, f"hidden{LAST}")
         quantise_wd(0, "wd_codes0", late[:, 3 * QUARTER + N :])

@@ -228,13 +228,16 @@ def tile_list_expert_dispatch_down_kernel(
                 sums.rearrange("t (c p u e) -> t c u p e", p=QUADRANT, u=2, e=2),
             )
 
-        def group_z(b, q, bank):
+        def turn_back(b, q, bank):
             part, m = divmod(q, 4 // Z_PARTS[b])
             words = z_turned[b, part][:].bitcast(F32).rearrange("t (c u p) -> t c u p", p=P, u=2)
             for c in range(2):
                 for u in range(2):
                     col = P * (2 * c + u)
                     nc.tensor.transpose(bank[:, col : col + P], words[:, 2 * m + c, u, :], ident[:])
+
+        def group_z(b, q, bank):
+            part, m = divmod(q, 4 // Z_PARTS[b])
             if m == 0:
                 width = 2 * T2 // Z_PARTS[b]
                 z_grouped[b, part] = keep.tile([P, width], F32, name=f"z_grouped{b}_{part}", align_bytes=64)
@@ -267,8 +270,8 @@ def tile_list_expert_dispatch_down_kernel(
             wd_plane[b] = plane
             nc.vector.quantize_mx(out=wd_codes[b][:].bitcast(FP8X4), scales=plane, in_=wd_grouped[b][:])
 
-        def down_pass(pair, b, q):
-            for n in range(N // P):
+        def down_pass(pair, b, q, row_tiles=range(N // P)):
+            for n in row_tiles:
                 cols = slice(P * n, P * (n + 1))
                 nc.tensor.matmul_mx(
                     out=pair[n // 2][:, QUARTER * (n % 2) : QUARTER * (n % 2 + 1)],
@@ -282,12 +285,11 @@ def tile_list_expert_dispatch_down_kernel(
 
         emptied_by = ((on_vector, on_vector), (on_scalar, on_scalar), (on_vector, on_scalar), (on_vector, on_scalar))
 
-        def store(pair, q):
-            for m, copy in enumerate(emptied_by[q]):
-                result = keep.tile([P, 2, QUARTER], F32, name=f"result{q}_{m}", tag=f"base{2 * q + m}")
-                copy(result[:].rearrange("p n t -> p (n t)"), pair[m][:])
-                rows = out[2 * P * m : 2 * P * (m + 1), QUARTER * q : QUARTER * (q + 1)]
-                nc.sync.dma_start(rows.rearrange("(n p) t -> p n t", n=2), result[:])
+        def store(pair, q, m):
+            result = keep.tile([P, 2, QUARTER], F32, name=f"result{q}_{m}", tag=f"base{2 * q + m}")
+            emptied_by[q][m](result[:].rearrange("p n t -> p (n t)"), pair[m][:])
+            rows = out[2 * P * m : 2 * P * (m + 1), QUARTER * q : QUARTER * (q + 1)]
+            nc.sync.dma_start(rows.rearrange("(n p) t -> p n t", n=2), result[:])
 
         def new_plane(name, width, tag):
             return keep.tile([P, width], U8, name=name, tag=tag, align_bytes=64)[:]
@@ -370,6 +372,7 @@ def tile_list_expert_dispatch_down_kernel(
                 sum_and_round(3)
             if i == 5:
                 for q in range(4):
+                    turn_back(0, q, spare_pair[q % 2])
                     group_z(0, q, spare_pair[q % 2])
                 gate_ahead(LAST)
                 sum_and_round(4)
@@ -384,24 +387,28 @@ def tile_list_expert_dispatch_down_kernel(
         turn_into(late_banks, pages[LAST % PAGES], False)
         late = new_plane("late_planes", 3 * QUARTER + 2 * N, f"hidden{LAST}")
         quantise_wd(0, "wd_codes0", late[:, 3 * QUARTER + N :])
-        down_pass(out_pairs[0], 0, 0)
+        down_pass(out_pairs[0], 0, 0, range(2))
         quantise_wd(1, "wd_codes1", late[:, 3 * QUARTER : 3 * QUARTER + N])
         for q in range(4):
             round_z(LAST, q, late_banks[q][:, :QUARTER], on_scalar)
         quantise_z(0, 1, 2, late[:, 2 * QUARTER : 3 * QUARTER])
 
         def finish(q):
-            if q >= 1:
-                down_pass(out_pairs[q], 0, q)
-            down_pass(out_pairs[q], 1, q)
-            store(out_pairs[q], q)
+            for m in range(2):
+                row_tiles = range(2 * m, 2 * m + 2)
+                if q >= 1:
+                    down_pass(out_pairs[q], 0, q, row_tiles)
+                down_pass(out_pairs[q], 1, q, row_tiles)
+                store(out_pairs[q], q, m)
 
+        for q in range(4):
+            turn_back(1, q, late_banks[q])
+        down_pass(out_pairs[0], 0, 0, range(2, 4))
         for q in range(4):
             group_z(1, q, late_banks[q])
             quantise_z(1, q, q + 1, new_plane(f"z_plane1_{q}", QUARTER, f"z_plane1_{q}"))
             if q == 1:
-                quantise_z(0, 2, 4, late[:, : 2 * QUARTER])
-            if q == 2:
                 finish(0)
+                quantise_z(0, 2, 4, late[:, : 2 * QUARTER])
         for q in range(1, 4):
             finish(q)

@@ -45,8 +45,9 @@ def tile_list_expert_dispatch_down_kernel(
         psum = ctx.enter_context(tc.psum_pool(name="psum", bufs=1))
 
         banks = [psum.tile([P, BANK], F32, name=f"bank{b}") for b in range(8)]
-        up_bank, gate_bank = banks[0], banks[1]
-        sum_pairs, spare_pair, late_banks = (banks[2:4], banks[4:6]), banks[6:8], banks[4:8]
+        pairs, gate_bank, spare_bank = (banks[0:2], banks[2:4], banks[4:6]), banks[6], banks[7]
+        early_banks = pairs[2] + pairs[0]
+        late_banks = [pairs[1][1], spare_bank] + pairs[2]
 
         idx = lists.tile([P, S // 16], U16, name="idx")
         idx2 = lists.tile([P, S // 16], U16, name="idx2")
@@ -119,17 +120,19 @@ def tile_list_expert_dispatch_down_kernel(
         load_wg_plane(WG_CHUNKS[1][0], ROW_TILES)
         load_wu(WU_CHUNKS[3])
         load_base(0)
-        load_wg(*WG_CHUNKS[2])
-        load_wu(WU_CHUNKS[4])
         load_base(1)
-        load_wd(0)
+        load_wg(*WG_CHUNKS[2])
         load_base(2)
+        load_wu(WU_CHUNKS[4])
+        load_base(3)
+        load_wd(0)
+        load_base(4)
         load_wd(1)
-        for i in range(3, ROW_TILES):
+        for i in range(5, ROW_TILES):
             load_base(i)
 
-        pages = [keep.tile([P, T2], F32, name=f"page{n}") for n in range(PAGES)]
-        ident = keep.tile([P, P], F32, name="ident")
+        pages = [keep.tile([P, T2], F32, name=f"page{n}", tag=f"page{n}", align_bytes=64) for n in range(PAGES)]
+        ident = keep.tile([P, P], F32, name="ident", tag="ident", align_bytes=64)
         nc.vector.memset(ident[:], 0.0)
         make_identity(nc, ident[:], nomemset=True)
         for page in pages:
@@ -190,7 +193,7 @@ def tile_list_expert_dispatch_down_kernel(
 
         def up_product(i):
             for a in range(PASSES):
-                up_pass(i, a, up_bank[:], slice(0, S))
+                up_pass(i, a, pairs[i % 3][0][:], slice(0, S))
 
         def new_gate(i):
             gates[i] = keep.tile([P, S], F32, name=f"gate{i}", tag=f"gate{i % GATES}", align_bytes=64)
@@ -199,7 +202,7 @@ def tile_list_expert_dispatch_down_kernel(
             new_gate(i)
             nc.scalar.activation(gates[i][:], gate_bank[:], SILU)
 
-        def turn_into(group, rows, opens):
+        def turn_into(group, rows, opens, identity=ident):
             blocks = T2 // P // len(group)
             for place, bank in enumerate(group):
                 for c in range(blocks):
@@ -207,7 +210,7 @@ def tile_list_expert_dispatch_down_kernel(
                     nc.tensor.matmul(
                         bank[:, P * c : P * (c + 1)],
                         lhsT=rows[:, t0 : t0 + P],
-                        rhs=ident[:],
+                        rhs=identity[:],
                         is_transpose=True,
                         start=(opens and c == 0),
                         stop=(not opens and c == blocks - 1),
@@ -228,13 +231,13 @@ def tile_list_expert_dispatch_down_kernel(
                 sums.rearrange("t (c p u e) -> t c u p e", p=QUADRANT, u=2, e=2),
             )
 
-        def turn_back(b, q, bank):
+        def turn_back(b, q, bank, identity):
             part, m = divmod(q, 4 // Z_PARTS[b])
             words = z_turned[b, part][:].bitcast(F32).rearrange("t (c u p) -> t c u p", p=P, u=2)
             for c in range(2):
                 for u in range(2):
                     col = P * (2 * c + u)
-                    nc.tensor.transpose(bank[:, col : col + P], words[:, 2 * m + c, u, :], ident[:])
+                    nc.tensor.transpose(bank[:, col : col + P], words[:, 2 * m + c, u, :], identity[:])
 
         def group_z(b, q, bank):
             part, m = divmod(q, 4 // Z_PARTS[b])
@@ -247,36 +250,34 @@ def tile_list_expert_dispatch_down_kernel(
                 bank[:].rearrange("p (c u t) -> p c t u", c=2, u=2),
             )
 
-        def quantise_z(b, first, end, plane, tag=None):
+        def quantise_z(b, first, end, codes, plane):
             part, m = divmod(first, 4 // Z_PARTS[b])
-            name = f"z_codes{b}_{first}"
-            codes = keep.tile([P, QUARTER * (end - first)], U32, name=name, tag=tag or name, align_bytes=64)
             words = z_grouped[b, part][:, 2 * QUARTER * m : 2 * QUARTER * (m + end - first)]
-            nc.vector.quantize_mx(out=codes[:].bitcast(FP8X4), scales=plane, in_=words.bitcast(BF16))
+            nc.vector.quantize_mx(out=codes.bitcast(FP8X4), scales=plane, in_=words.bitcast(BF16))
             for q in range(first, end):
                 cols = slice(QUARTER * (q - first), QUARTER * (q - first + 1))
                 z_codes[b, q], z_plane[b, q] = codes[:, cols], plane[:, cols]
 
-        wd_grouped = [keep.tile([P, N * SLOTS], BF16, name=f"wd_grouped{b}", align_bytes=64) for b in range(PASSES)]
-        wd_codes, wd_plane = {}, {}
+        wd_grouped, wd_codes, wd_plane = {}, {}, {}
 
-        def group_wd(b, h):
-            target = wd_grouped[b][:].rearrange("p (h c w j) -> p h c j w", h=2, w=4, j=SLOTS)
+        def group_wd(b, h, tag):
+            wd_grouped[b, h] = keep.tile([P, N * SLOTS // 2], BF16, name=f"wd_grouped{b}_{h}", tag=tag, align_bytes=64)
+            target = wd_grouped[b, h][:].rearrange("p (c w j) -> p c j w", w=4, j=SLOTS)
             source = wd_raw[b][:].rearrange("p j (h c w) -> p h c j w", h=2, w=4)
-            on_scalar(target[:, h], source[:, h])
+            on_scalar(target, source[:, h])
 
-        def quantise_wd(b, tag, plane):
-            wd_codes[b] = keep.tile([P, N], U32, name=f"wd_codes{b}", tag=tag, align_bytes=64)
-            wd_plane[b] = plane
-            nc.vector.quantize_mx(out=wd_codes[b][:].bitcast(FP8X4), scales=plane, in_=wd_grouped[b][:])
+        def quantise_wd(b, h, codes, plane):
+            nc.vector.quantize_mx(out=codes.bitcast(FP8X4), scales=plane, in_=wd_grouped[b, h][:])
+            for m in range(2):
+                cols = slice(P * m, P * (m + 1))
+                wd_codes[b, 2 * h + m], wd_plane[b, 2 * h + m] = codes[:, cols], plane[:, cols]
 
         def down_pass(pair, b, q, row_tiles=range(N // P)):
             for n in row_tiles:
-                cols = slice(P * n, P * (n + 1))
                 nc.tensor.matmul_mx(
                     out=pair[n // 2][:, QUARTER * (n % 2) : QUARTER * (n % 2 + 1)],
-                    lhsT=wd_codes[b][:, cols].bitcast(FP8X4),
-                    lhsT_scale=wd_plane[b][:, cols],
+                    lhsT=wd_codes[b, n].bitcast(FP8X4),
+                    lhsT_scale=wd_plane[b, n],
                     rhs=z_codes[b, q].bitcast(FP8X4),
                     rhs_scale=z_plane[b, q],
                     start=(b == 0 and n % 2 == 0),
@@ -291,11 +292,14 @@ def tile_list_expert_dispatch_down_kernel(
             rows = out[2 * P * m : 2 * P * (m + 1), QUARTER * q : QUARTER * (q + 1)]
             nc.sync.dma_start(rows.rearrange("(n p) t -> p n t", n=2), result[:])
 
+        def new_codes(name, width, tag):
+            return keep.tile([P, width], U32, name=name, tag=tag, align_bytes=64)[:]
+
         def new_plane(name, width, tag):
             return keep.tile([P, width], U8, name=name, tag=tag, align_bytes=64)[:]
 
         def sum_and_round(i):
-            sum_pair = sum_pairs[i % 2]
+            sum_pair = pairs[i % 3]
             turn_into(sum_pair, base_rows[i], True)
             turn_into(sum_pair, pages[i % PAGES], False)
             parts = Z_PARTS[i // TILES_PER_PASS]
@@ -315,12 +319,12 @@ def tile_list_expert_dispatch_down_kernel(
                     places = idx[:, entries.start // 16 : entries.stop // 16]
                     nc.vector.tensor_copy(v_codes[a][:, entries], table[a][:].bitcast(U32).indirect(places))
                 for m in range(2):
-                    target = late_banks[n][:, P * m : P * (m + 1)]
+                    target = early_banks[n][:, P * m : P * (m + 1)]
                     quarter = slice(entries.start + P * m, entries.start + P * (m + 1))
                     gate_pass(0, a, target, quarter, a == 0 and m == 0, a == PASSES - 1 and m == 1)
-                up_pass(0, a, late_banks[2 + n][:, :half], entries)
+                up_pass(0, a, early_banks[2 + n][:, :half], entries)
                 if a == PASSES - 1:
-                    nc.scalar.activation(gates[0][:, entries], late_banks[n][:, :half], SILU)
+                    nc.scalar.activation(gates[0][:, entries], early_banks[n][:, :half], SILU)
         gate_product(1)
 
         def scatter(i, hidden, first, end):
@@ -328,7 +332,7 @@ def tile_list_expert_dispatch_down_kernel(
             nc.vector.tensor_tensor(pages[i % PAGES][:].indirect(places), hidden, weights[:, first:end], MULT)
 
         early = keep.tile([P, half], F32, name="hidden_early")
-        nc.vector.tensor_tensor(early[:], late_banks[2][:, :half], gates[0][:, :half], MULT)
+        nc.vector.tensor_tensor(early[:], early_banks[2][:, :half], gates[0][:, :half], MULT)
         scatter(0, early[:], 0, half)
 
         def gate_ahead(i):
@@ -342,56 +346,74 @@ def tile_list_expert_dispatch_down_kernel(
                 if i == 1:
                     gate_ahead(1)
                 group_wu(WU_CHUNKS[i + 1])
+            if i in (0, 1, 3, 5):
                 tag = f"wu_raw{i + 1}_{PASSES - 1}"
             first = half if i == 0 else 0
             hidden = keep.tile([P, S - first], F32, name=f"hidden{i}", tag=tag, align_bytes=64)
-            product = late_banks[3][:, :half] if i == 0 else up_bank[:]
+            product = early_banks[3][:, :half] if i == 0 else pairs[i % 3][0][:]
             nc.vector.tensor_tensor(hidden[:], product, gates[i][:, first:], MULT)
             if i < LAST:
                 quantise_wu(i + 1)
                 up_product(i + 1)
             else:
-                quantise_z(0, 0, 1, new_plane("z_plane0_0", QUARTER, "z_plane0_0"), "weight_codes")
+                codes = new_codes("z_codes0_0", QUARTER, "weight_codes")
+                quantise_z(0, 0, 1, codes, new_plane("z_plane0_0", QUARTER, "z_plane0_0"))
             scatter(i, hidden[:], first, S)
             if 1 <= i <= 4:
                 gate_ahead(i + 1)
+            if 1 <= i < LAST:
+                sum_and_round(i - 1)
             if i == 1:
                 group_wu(WU_CHUNKS[3])
-            if i == 2:
-                sum_and_round(0)
-                group_wu(WU_CHUNKS[4])
             if i == 3:
-                sum_and_round(1)
-                for h in range(2):
-                    group_wd(0, h)
+                group_wu(WU_CHUNKS[4])
             if i == 4:
-                sum_and_round(2)
-                for h in range(2):
-                    group_wd(1, h)
                 gate_ahead(6)
-                sum_and_round(3)
+                group_wd(0, 0, "wd_grouped0_0")
+                group_wd(1, 0, "wd_grouped1_0")
+            if i == 6:
+                group_wd(1, 1, "wd_grouped1_1")
             if i == 5:
                 for q in range(4):
-                    turn_back(0, q, spare_pair[q % 2])
-                    group_z(0, q, spare_pair[q % 2])
+                    bank = (spare_bank, pairs[0][1])[q % 2]
+                    turn_back(0, q, bank, ident)
+                    group_z(0, q, bank)
                 gate_ahead(LAST)
-                sum_and_round(4)
-            if i == 6:
-                sum_and_round(5)
 
-        sum_and_round(LAST - 1)
+        def warm_up(bank, widths):
+            for n, width in enumerate(widths):
+                gate_pass(LAST, 0, bank[:, :width], slice(0, width), n == 0, n == len(widths) - 1)
+
+        sum_pair, last_up_bank = pairs[(LAST - 1) % 3], pairs[LAST % 3][0]
+        turn_into(sum_pair, base_rows[LAST - 1], True)
         turn_into(late_banks, base_rows[LAST], True)
-        out_pairs = [[up_bank, gate_bank], sum_pairs[0], late_banks[0:2], late_banks[2:4]]
-        for n in range(4):
-            gate_pass(LAST, n % PASSES, up_bank[:], slice(0, S), n == 0, n == 3)
-        turn_into(late_banks, pages[LAST % PAGES], False)
-        late = new_plane("late_planes", 3 * QUARTER + 2 * N, f"hidden{LAST}")
-        quantise_wd(0, "wd_codes0", late[:, 3 * QUARTER + N :])
+        turn_into(sum_pair, pages[(LAST - 1) % PAGES], False)
+        warm_up(last_up_bank, (S, S))
+        group_wd(0, 1, f"page{(LAST - 1) % PAGES}")
+        for q in range(4):
+            first = QUARTER * (q % 2)
+            round_z(LAST - 1, q, sum_pair[q // 2][:, first : first + QUARTER], on_scalar)
+            if q % 2 == 1:
+                warm_up(sum_pair[q // 2], (S, P, P, P) if q == 1 else (S,))
+        late_ident = keep.tile([P, P], F32, name="late_ident", tag="wd_raw0", align_bytes=64)
+        on_scalar(late_ident[:], ident[:])
+        turn_into(late_banks, pages[LAST % PAGES], False, late_ident)
+        out_pairs = [[last_up_bank, gate_bank], sum_pair, late_banks[0:2], late_banks[2:4]]
+        late_planes = new_plane("late_planes", 7 * QUARTER, f"hidden{LAST}")
+        late_codes = new_codes("late_codes", 7 * QUARTER, "ident")
+
+        def late(first, end):
+            cols = slice(QUARTER * first, QUARTER * end)
+            return late_codes[:, cols], late_planes[:, cols]
+
+        quantise_wd(0, 0, *late(0, 1))
         down_pass(out_pairs[0], 0, 0, range(2))
-        quantise_wd(1, "wd_codes1", late[:, 3 * QUARTER : 3 * QUARTER + N])
+        quantise_wd(1, 0, *late(1, 2))
+        quantise_wd(0, 1, *late(2, 3))
+        quantise_wd(1, 1, *late(3, 4))
         for q in range(4):
             round_z(LAST, q, late_banks[q][:, :QUARTER], on_scalar)
-        quantise_z(0, 1, 2, late[:, 2 * QUARTER : 3 * QUARTER])
+        quantise_z(0, 1, 2, *late(4, 5))
 
         def finish(q):
             for m in range(2):
@@ -402,13 +424,14 @@ def tile_list_expert_dispatch_down_kernel(
                 store(out_pairs[q], q, m)
 
         for q in range(4):
-            turn_back(1, q, late_banks[q])
+            turn_back(1, q, late_banks[q], late_ident)
         down_pass(out_pairs[0], 0, 0, range(2, 4))
         for q in range(4):
             group_z(1, q, late_banks[q])
-            quantise_z(1, q, q + 1, new_plane(f"z_plane1_{q}", QUARTER, f"z_plane1_{q}"))
+            codes = new_codes(f"z_codes1_{q}", QUARTER, f"z_codes1_{q}")
+            quantise_z(1, q, q + 1, codes, new_plane(f"z_plane1_{q}", QUARTER, f"z_plane1_{q}"))
             if q == 1:
                 finish(0)
-                quantise_z(0, 2, 4, late[:, : 2 * QUARTER])
+                quantise_z(0, 2, 4, *late(5, 7))
         for q in range(1, 4):
             finish(q)

@@ -260,17 +260,21 @@ def tile_list_expert_dispatch_down_kernel(
 
         wd_grouped, wd_codes, wd_plane = {}, {}, {}
 
-        def group_wd(b, h, tag):
-            wd_grouped[b, h] = keep.tile([P, N * SLOTS // 2], BF16, name=f"wd_grouped{b}_{h}", tag=tag, align_bytes=64)
-            target = wd_grouped[b, h][:].rearrange("p (c w j) -> p c j w", w=4, j=SLOTS)
-            source = wd_raw[b][:].rearrange("p j (h c w) -> p h c j w", h=2, w=4)
-            on_scalar(target, source[:, h])
+        def group_wd(b, first, end, tag=None):
+            name = f"wd_grouped{b}_{first}"
+            width = K_PASS * (end - first)
+            wd_grouped[b, first] = keep.tile([P, width], BF16, name=name, tag=tag or name, align_bytes=64)
+            target = wd_grouped[b, first][:].rearrange("p (c w j) -> p c j w", w=4, j=SLOTS)
+            source = wd_raw[b][:, :, P * first : P * end].rearrange("p j (c w) -> p c j w", w=4)
+            on_scalar(target, source)
 
-        def quantise_wd(b, h, codes, plane):
-            nc.vector.quantize_mx(out=codes.bitcast(FP8X4), scales=plane, in_=wd_grouped[b, h][:])
-            for m in range(2):
-                cols = slice(P * m, P * (m + 1))
-                wd_codes[b, 2 * h + m], wd_plane[b, 2 * h + m] = codes[:, cols], plane[:, cols]
+        def quantise_wd(b, first, end):
+            place = N * b + P * first
+            codes, plane = late(place, place + P * (end - first))
+            nc.vector.quantize_mx(out=codes.bitcast(FP8X4), scales=plane, in_=wd_grouped[b, first][:])
+            for n in range(first, end):
+                cols = slice(P * (n - first), P * (n - first + 1))
+                wd_codes[b, n], wd_plane[b, n] = codes[:, cols], plane[:, cols]
 
         def down_pass(pair, b, q, row_tiles=range(N // P)):
             for n in row_tiles:
@@ -369,10 +373,11 @@ def tile_list_expert_dispatch_down_kernel(
                 group_wu(WU_CHUNKS[4])
             if i == 4:
                 gate_ahead(6)
-                group_wd(0, 0, "wd_grouped0_0")
-                group_wd(1, 0, "wd_grouped1_0")
+                group_wd(0, 0, 2)
+                group_wd(0, 2, 4)
             if i == 6:
-                group_wd(1, 1, "wd_grouped1_1")
+                group_wd(1, 0, 2)
+                group_wd(1, 2, 3)
             if i == 5:
                 for q in range(4):
                     bank = (spare_bank, pairs[0][1])[q % 2]
@@ -388,14 +393,14 @@ def tile_list_expert_dispatch_down_kernel(
         turn_into(sum_pair, base_rows[LAST - 1], True)
         turn_into(late_banks, base_rows[LAST], True)
         turn_into(sum_pair, pages[(LAST - 1) % PAGES], False)
-        warm_up(last_up_bank, (S, S))
-        group_wd(0, 1, f"page{(LAST - 1) % PAGES}")
+        warm_up(last_up_bank, (S, P, P, P))
+        group_wd(1, 3, 4, f"page{(LAST - 1) % PAGES}")
         for q in range(4):
             first = QUARTER * (q % 2)
             round_z(LAST - 1, q, sum_pair[q // 2][:, first : first + QUARTER], on_scalar)
             if q % 2 == 1:
-                warm_up(sum_pair[q // 2], (S, P, P, P) if q == 1 else (S,))
-        late_ident = keep.tile([P, P], F32, name="late_ident", tag="wd_raw0", align_bytes=64)
+                warm_up(sum_pair[q // 2], (S,) if q == 1 else (S, S))
+        late_ident = keep.tile([P, P], F32, name="late_ident", tag="wd_raw1", align_bytes=64)
         on_scalar(late_ident[:], ident[:])
         turn_into(late_banks, pages[LAST % PAGES], False, late_ident)
         out_pairs = [[last_up_bank, gate_bank], sum_pair, late_banks[0:2], late_banks[2:4]]
@@ -403,17 +408,17 @@ def tile_list_expert_dispatch_down_kernel(
         late_codes = new_codes("late_codes", 7 * QUARTER, "ident")
 
         def late(first, end):
-            cols = slice(QUARTER * first, QUARTER * end)
-            return late_codes[:, cols], late_planes[:, cols]
+            return late_codes[:, first:end], late_planes[:, first:end]
 
-        quantise_wd(0, 0, *late(0, 1))
-        down_pass(out_pairs[0], 0, 0, range(2))
-        quantise_wd(1, 0, *late(1, 2))
-        quantise_wd(0, 1, *late(2, 3))
-        quantise_wd(1, 1, *late(3, 4))
+        quantise_wd(0, 0, 2)
+        quantise_wd(0, 2, 4)
+        down_pass(out_pairs[0], 0, 0)
+        quantise_wd(1, 0, 2)
+        quantise_wd(1, 2, 3)
+        quantise_wd(1, 3, 4)
         for q in range(4):
             round_z(LAST, q, late_banks[q][:, :QUARTER], on_scalar)
-        quantise_z(0, 1, 2, *late(4, 5))
+        quantise_z(0, 1, 2, *late(2 * N, 2 * N + QUARTER))
 
         def finish(q):
             for m in range(2):
@@ -425,13 +430,12 @@ def tile_list_expert_dispatch_down_kernel(
 
         for q in range(4):
             turn_back(1, q, late_banks[q], late_ident)
-        down_pass(out_pairs[0], 0, 0, range(2, 4))
         for q in range(4):
             group_z(1, q, late_banks[q])
             codes = new_codes(f"z_codes1_{q}", QUARTER, f"z_codes1_{q}")
             quantise_z(1, q, q + 1, codes, new_plane(f"z_plane1_{q}", QUARTER, f"z_plane1_{q}"))
             if q == 1:
                 finish(0)
-                quantise_z(0, 2, 4, *late(5, 7))
+                quantise_z(0, 2, 4, *late(2 * N + QUARTER, 2 * N + 3 * QUARTER))
         for q in range(1, 4):
             finish(q)

@@ -373,17 +373,17 @@ def tile_list_expert_dispatch_down_kernel(
                 group_wu(WU_CHUNKS[4])
             if i == 4:
                 gate_ahead(6)
-                group_wd(0, 0, 2)
-                group_wd(0, 2, 4)
-            if i == 6:
-                group_wd(1, 0, 2)
-                group_wd(1, 2, 3)
-            if i == 5:
                 for q in range(4):
                     bank = (spare_bank, pairs[0][1])[q % 2]
                     turn_back(0, q, bank, ident)
                     group_z(0, q, bank)
+            if i == 6:
+                group_wd(1, 0, 2)
+                group_wd(1, 2, 3)
+            if i == 5:
                 gate_ahead(LAST)
+                group_wd(0, 0, 2)
+                group_wd(0, 2, 4)
 
         def warm_up(bank, widths):
             for n, width in enumerate(widths):
@@ -423,13 +423,14 @@ def tile_list_expert_dispatch_down_kernel(
         def finish(q):
             for m in range(2):
                 row_tiles = range(2 * m, 2 * m + 2)
-                if q >= 1:
+                if 2 * q + m >= 3:
                     down_pass(out_pairs[q], 0, q, row_tiles)
                 down_pass(out_pairs[q], 1, q, row_tiles)
                 store(out_pairs[q], q, m)
 
         for q in range(4):
             turn_back(1, q, late_banks[q], late_ident)
+        down_pass(out_pairs[1], 0, 1, range(2))
         for q in range(4):
             group_z(1, q, late_banks[q])
             codes = new_codes(f"z_codes1_{q}", QUARTER, f"z_codes1_{q}")

@@ -30,6 +30,8 @@ QUARTER = T2 // 4
 PAGES = 3
 GATES = 3
 WU_CHUNKS = ((0,), (1,), (2, 3), (4, 5), (6, 7))
+SHARE = P
+FIRST_SHARED = 2
 WG_CHUNKS = ((0, 2), (2, 4), (4, 8))
 Z_PARTS = (2, 4)
 
@@ -159,7 +161,7 @@ def tile_list_expert_dispatch_down_kernel(
 
         def quantise_wu(i):
             codes = keep.tile([P, PASSES * P], U32, name=f"wu_codes{i}", tag="weight_codes", align_bytes=64)
-            plane = keep.tile([P, PASSES * P], U8, name=f"wu_plane{i}", align_bytes=64)
+            plane = keep.tile([P, PASSES * P], U8, name=f"wu_plane{i}", tag=f"aside{i - 1}", align_bytes=64)
             nc.vector.quantize_mx(out=codes[:].bitcast(FP8X4), scales=plane[:], in_=wu_grouped[i])
             for a in range(PASSES):
                 cols = slice(P * a, P * (a + 1))
@@ -191,9 +193,14 @@ def tile_list_expert_dispatch_down_kernel(
             for a in range(PASSES):
                 gate_pass(i, a, gate_bank[:], slice(0, S), a == 0, a == PASSES - 1)
 
+        aside = {}
+
         def up_product(i):
             for a in range(PASSES):
                 up_pass(i, a, pairs[i % 3][0][:], slice(0, S))
+            if i >= FIRST_SHARED:
+                aside[i] = keep.tile([P, SHARE], F32, name=f"aside{i}", tag=f"aside{i}", align_bytes=64)
+                on_scalar(aside[i][:], pairs[i % 3][0][:, S - SHARE :])
 
         def new_gate(i):
             gates[i] = keep.tile([P, S], F32, name=f"gate{i}", tag=f"gate{i % GATES}", align_bytes=64)
@@ -354,14 +361,19 @@ def tile_list_expert_dispatch_down_kernel(
                 tag = f"wu_raw{i + 1}_{PASSES - 1}"
             first = half if i == 0 else 0
             hidden = keep.tile([P, S - first], F32, name=f"hidden{i}", tag=tag, align_bytes=64)
-            product = early_banks[3][:, :half] if i == 0 else pairs[i % 3][0][:]
-            nc.vector.tensor_tensor(hidden[:], product, gates[i][:, first:], MULT)
+            if i < FIRST_SHARED:
+                product = early_banks[3][:, :half] if i == 0 else pairs[i % 3][0][:]
+                nc.vector.tensor_tensor(hidden[:], product, gates[i][:, first:], MULT)
+            else:
+                cut = S - SHARE
+                nc.vector.tensor_tensor(hidden[:, :cut], pairs[i % 3][0][:, :cut], gates[i][:, :cut], MULT)
+                nc.gpsimd.tensor_tensor(hidden[:, cut:], aside[i][:], gates[i][:, cut:], MULT)
             if i < LAST:
                 quantise_wu(i + 1)
                 up_product(i + 1)
             else:
                 codes = new_codes("z_codes0_0", QUARTER, "weight_codes")
-                quantise_z(0, 0, 1, codes, new_plane("z_plane0_0", QUARTER, "z_plane0_0"))
+                quantise_z(0, 0, 1, codes, new_plane("z_plane0_0", QUARTER, f"aside{LAST}"))
             scatter(i, hidden[:], first, S)
             if 1 <= i <= 4:
                 gate_ahead(i + 1)

@@ -22,6 +22,7 @@ SLOTS = 4
 K_PASS = P * SLOTS
 PASSES = 2
 QUADRANT = 32
+SPREAD = 8
 BANK = 512
 ROW_TILES = H // P
 LAST = ROW_TILES - 1
@@ -74,15 +75,15 @@ def tile_list_expert_dispatch_down_kernel(
                     col = width * a + P * (i - first)
                     wg_plane[i, a] = plane[:, col : col + P]
 
-        tab_plane = keep.tile([P, PASSES * T], U8, name="tab_plane", align_bytes=64)
+        tab_plane = keep.tile([P, PASSES * T], U8, name="tab_plane", tag="tab_plane", align_bytes=64)
         nc.vector.memset(tab_plane[:].bitcast(I32), 0)
 
         table = [keep.tile([P, T], I32, name=f"table{a}", align_bytes=64) for a in range(PASSES)]
         wu_raw, wg_codes, base_rows, wd_raw = {}, {}, {}, {}
 
-        def load_wu(chunk):
+        def load_wu(chunk, passes=range(PASSES)):
             width = P * len(chunk)
-            for a in range(PASSES):
+            for a in passes:
                 tag = f"wu_raw{chunk[0]}_{a}"
                 wu_raw[chunk, a] = keep.tile([P, SLOTS, width], F32, name=tag, tag=tag, align_bytes=64)
                 rows = wu[K_PASS * a : K_PASS * (a + 1), P * chunk[0] : P * chunk[0] + width]
@@ -107,16 +108,33 @@ def tile_list_expert_dispatch_down_kernel(
         def load_table(a):
             nc.sync.dma_start(table[a][:], tab_words[a].rearrange("p t i -> p (t i)").bitcast(I32))
 
-        load_wu(WU_CHUNKS[0])
-        load_plane(tab_plane, tab_scales)
+        load_wu(WU_CHUNKS[0], [0])
+        nc.sync.dma_start(
+            tab_plane[0:P:SPREAD, :].bitcast(I32).rearrange("q (a c) -> q a c", a=PASSES),
+            tab_scales.bitcast(I32).rearrange("a q c -> q a c"),
+        )
+        load_wu(WU_CHUNKS[0], [1])
         load_table(0)
         load_wg(*WG_CHUNKS[0])
         load_wg_plane(*WG_CHUNKS[0])
         load_table(1)
-        nc.sync.dma_start(idx2[:], offs2)
+
+        ident = keep.tile([P, P], F32, name="ident", tag="ident", align_bytes=64)
+        nc.vector.memset(ident[:], 0.0)
+        make_identity(nc, ident[:], nomemset=True)
+        picked = keep.tile([P, PASSES * S], U8, name="picked", align_bytes=64)
+        moved = keep.tile([P, PASSES * S], U8, name="moved", align_bytes=64)
+        v_plane = [moved[:, S * a : S * (a + 1)] for a in range(PASSES)]
+        v_codes = [keep.tile([P, S], U32, name=f"v_codes{a}", align_bytes=64) for a in range(PASSES)]
+        for a in range(PASSES):
+            nc.vector.tensor_copy(picked[:, S * a : S * (a + 1)], tab_plane[:, T * a : T * (a + 1)].indirect(idx[:]))
+        for r in range(4):
+            nc.sync.dma_start(moved[r:P:QUADRANT, :].bitcast(I32), picked[SPREAD * r : P : QUADRANT, :].bitcast(I32))
+        nc.vector.tensor_copy(v_codes[0][:], table[0][:].bitcast(U32).indirect(idx[:]))
         weights = keep.tile([P, S], F32, name="weights")
         nc.sync.dma_start(weights[:], wgs)
         load_wu(WU_CHUNKS[1])
+        nc.sync.dma_start(idx2[:], offs2)
         load_wu(WU_CHUNKS[2])
         load_wg(*WG_CHUNKS[1])
         load_wg_plane(WG_CHUNKS[1][0], ROW_TILES)
@@ -133,18 +151,11 @@ def tile_list_expert_dispatch_down_kernel(
         for i in range(5, ROW_TILES):
             load_base(i)
 
-        pages = [keep.tile([P, T2], F32, name=f"page{n}", tag=f"page{n}", align_bytes=64) for n in range(PAGES)]
-        ident = keep.tile([P, P], F32, name="ident", tag="ident", align_bytes=64)
-        nc.vector.memset(ident[:], 0.0)
-        make_identity(nc, ident[:], nomemset=True)
+
+        tags = [f"page{n}" for n in range(PAGES - 1)] + ["tab_plane"]
+        pages = [keep.tile([P, T2], F32, name=f"page{n}", tag=tags[n], align_bytes=64) for n in range(PAGES)]
         for page in pages:
             nc.vector.memset(page[:], 0.0)
-
-        v_plane = [keep.tile([P, S], U8, name=f"v_plane{a}", align_bytes=64) for a in range(PASSES)]
-        v_codes = [keep.tile([P, S], U32, name=f"v_codes{a}", align_bytes=64) for a in range(PASSES)]
-        for a in range(PASSES):
-            nc.vector.tensor_copy(v_plane[a][:], tab_plane[:, T * a : T * (a + 1)].indirect(idx[:]))
-        nc.vector.tensor_copy(v_codes[0][:], table[0][:].bitcast(U32).indirect(idx[:]))
 
         wu_codes, wu_plane, gates = {}, {}, {}
 

@@ -30,7 +30,7 @@ TILES_PER_PASS = K_PASS // P
 QUARTER = T2 // 4
 PAGES = 3
 GATES = 3
-WU_CHUNKS = ((0,), (1,), (2, 3), (4, 5), (6, 7))
+WU_CHUNKS = ((0,), (1,), (2,), (3,), (4, 5), (6, 7))
 SHARE = P
 FIRST_SHARED = 2
 WG_CHUNKS = ((0, 2), (2, 4), (4, 8))
@@ -55,6 +55,7 @@ def tile_list_expert_dispatch_down_kernel(
         idx = lists.tile([P, S // 16], U16, name="idx")
         idx2 = lists.tile([P, S // 16], U16, name="idx2")
         nc.sync.dma_start(idx[:], offs)
+        nc.sync.dma_start(idx2[:], offs2)
 
         def load_plane(plane, scales):
             for r in range(4):
@@ -134,16 +135,16 @@ def tile_list_expert_dispatch_down_kernel(
         weights = keep.tile([P, S], F32, name="weights")
         nc.sync.dma_start(weights[:], wgs)
         load_wu(WU_CHUNKS[1])
-        nc.sync.dma_start(idx2[:], offs2)
         load_wu(WU_CHUNKS[2])
+        load_wu(WU_CHUNKS[3])
         load_wg(*WG_CHUNKS[1])
         load_wg_plane(WG_CHUNKS[1][0], ROW_TILES)
-        load_wu(WU_CHUNKS[3])
+        load_wu(WU_CHUNKS[4])
         load_base(0)
         load_base(1)
         load_wg(*WG_CHUNKS[2])
         load_base(2)
-        load_wu(WU_CHUNKS[4])
+        load_wu(WU_CHUNKS[5])
         load_base(3)
         load_wd(0)
         load_base(4)
@@ -368,7 +369,9 @@ def tile_list_expert_dispatch_down_kernel(
                 if i == 1:
                     gate_ahead(1)
                 group_wu(WU_CHUNKS[i + 1])
-            if i in (0, 1, 3, 5):
+                if i == 1:
+                    group_wu(WU_CHUNKS[3])
+            if i in (0, 1, 2, 3, 5):
                 tag = f"wu_raw{i + 1}_{PASSES - 1}"
             first = half if i == 0 else 0
             hidden = keep.tile([P, S - first], F32, name=f"hidden{i}", tag=tag, align_bytes=64)
@@ -391,9 +394,9 @@ def tile_list_expert_dispatch_down_kernel(
             if 1 <= i < LAST:
                 sum_and_round(i - 1)
             if i == 1:
-                group_wu(WU_CHUNKS[3])
-            if i == 3:
                 group_wu(WU_CHUNKS[4])
+            if i == 3:
+                group_wu(WU_CHUNKS[5])
             if i == 4:
                 gate_ahead(6)
                 for q in range(4):

@@ -32,7 +32,7 @@ PAGES = 3
 GATES = 3
 WU_CHUNKS = ((0,), (1,), (2,), (3,), (4, 5), (6, 7))
 SHARE = P
-FIRST_SHARED = 2
+FIRST_SHARED = 4
 WG_CHUNKS = ((0, 2), (2, 4), (4, 8))
 Z_PARTS = (2, 4)
 
@@ -132,9 +132,9 @@ def tile_list_expert_dispatch_down_kernel(
         for r in range(4):
             nc.sync.dma_start(moved[r:P:QUADRANT, :].bitcast(I32), picked[SPREAD * r : P : QUADRANT, :].bitcast(I32))
         nc.vector.tensor_copy(v_codes[0][:], table[0][:].bitcast(U32).indirect(idx[:]))
+        load_wu(WU_CHUNKS[1])
         weights = keep.tile([P, S], F32, name="weights")
         nc.sync.dma_start(weights[:], wgs)
-        load_wu(WU_CHUNKS[1])
         load_wu(WU_CHUNKS[2])
         load_wu(WU_CHUNKS[3])
         load_wg(*WG_CHUNKS[1])
@@ -258,13 +258,13 @@ def tile_list_expert_dispatch_down_kernel(
                     col = P * (2 * c + u)
                     nc.tensor.transpose(bank[:, col : col + P], words[:, 2 * m + c, u, :], identity[:])
 
-        def group_z(b, q, bank):
+        def group_z(b, q, bank, copy=on_scalar):
             part, m = divmod(q, 4 // Z_PARTS[b])
             if m == 0:
                 width = 2 * T2 // Z_PARTS[b]
                 z_grouped[b, part] = keep.tile([P, width], F32, name=f"z_grouped{b}_{part}", align_bytes=64)
             target = z_grouped[b, part][:, 2 * QUARTER * m : 2 * QUARTER * (m + 1)]
-            on_scalar(
+            copy(
                 target.rearrange("p (c t u) -> p c t u", c=2, u=2),
                 bank[:].rearrange("p (c u t) -> p c t u", c=2, u=2),
             )
@@ -336,18 +336,16 @@ def tile_list_expert_dispatch_down_kernel(
         half = S // 2
         halves = [slice(half * n, half * (n + 1)) for n in range(2)]
         new_gate(0)
-        for a in range(PASSES):
-            for n, entries in enumerate(halves):
-                if a == PASSES - 1:
-                    places = idx[:, entries.start // 16 : entries.stop // 16]
-                    nc.vector.tensor_copy(v_codes[a][:, entries], table[a][:].bitcast(U32).indirect(places))
-                for m in range(2):
-                    target = early_banks[n][:, P * m : P * (m + 1)]
-                    quarter = slice(entries.start + P * m, entries.start + P * (m + 1))
-                    gate_pass(0, a, target, quarter, a == 0 and m == 0, a == PASSES - 1 and m == 1)
+        for n, entries in enumerate(halves):
+            places = idx[:, entries.start // 16 : entries.stop // 16]
+            nc.vector.tensor_copy(v_codes[1][:, entries], table[1][:].bitcast(U32).indirect(places))
+            for a in range(PASSES):
+                gate_pass(0, a, early_banks[n][:, :half], entries, a == 0, a == PASSES - 1)
+            nc.scalar.activation(gates[0][:, entries], early_banks[n][:, :half], SILU)
+            if n == 0:
+                group_wu(WU_CHUNKS[1])
+            for a in range(PASSES):
                 up_pass(0, a, early_banks[2 + n][:, :half], entries)
-                if a == PASSES - 1:
-                    nc.scalar.activation(gates[0][:, entries], early_banks[n][:, :half], SILU)
         gate_product(1)
 
         def scatter(i, hidden, first, end):
@@ -368,8 +366,7 @@ def tile_list_expert_dispatch_down_kernel(
             if i <= 1:
                 if i == 1:
                     gate_ahead(1)
-                group_wu(WU_CHUNKS[i + 1])
-                if i == 1:
+                    group_wu(WU_CHUNKS[2])
                     group_wu(WU_CHUNKS[3])
             if i in (0, 1, 2, 3, 5):
                 tag = f"wu_raw{i + 1}_{PASSES - 1}"
@@ -444,7 +441,6 @@ def tile_list_expert_dispatch_down_kernel(
         quantise_wd(1, 3, 4)
         for q in range(4):
             round_z(LAST, q, late_banks[q][:, :QUARTER], on_scalar)
-        quantise_z(0, 1, 2, *late(2 * N, 2 * N + QUARTER))
 
         def finish(q):
             for m in range(2):
@@ -456,9 +452,11 @@ def tile_list_expert_dispatch_down_kernel(
 
         for q in range(4):
             turn_back(1, q, late_banks[q], late_ident)
-        down_pass(out_pairs[1], 0, 1, range(2))
         for q in range(4):
-            group_z(1, q, late_banks[q])
+            group_z(1, q, late_banks[q], on_vector if q == 0 else on_scalar)
+            if q == 0:
+                quantise_z(0, 1, 2, *late(2 * N, 2 * N + QUARTER))
+                down_pass(out_pairs[1], 0, 1, range(2))
             codes = new_codes(f"z_codes1_{q}", QUARTER, f"z_codes1_{q}")
             quantise_z(1, q, q + 1, codes, new_plane(f"z_plane1_{q}", QUARTER, f"z_plane1_{q}"))
             if q == 1:

@@ -32,7 +32,7 @@ PAGES = 3
 GATES = 3
 WU_CHUNKS = ((0,), (1,), (2,), (3,), (4, 5), (6, 7))
 SHARE = P
-FIRST_SHARED = 4
+SHARED = (2, 4, 6, 7)
 WG_CHUNKS = ((0, 2), (2, 4), (4, 8))
 Z_PARTS = (2, 4)
 
@@ -149,7 +149,7 @@ def tile_list_expert_dispatch_down_kernel(
         load_wd(0)
         load_base(4)
         load_wd(1)
-        for i in range(5, ROW_TILES):
+        for i in (LAST, 5, 6):
             load_base(i)
 
 
@@ -210,7 +210,7 @@ def tile_list_expert_dispatch_down_kernel(
         def up_product(i):
             for a in range(PASSES):
                 up_pass(i, a, pairs[i % 3][0][:], slice(0, S))
-            if i >= FIRST_SHARED:
+            if i in SHARED:
                 aside[i] = keep.tile([P, SHARE], F32, name=f"aside{i}", tag=f"aside{i}", align_bytes=64)
                 on_scalar(aside[i][:], pairs[i % 3][0][:, S - SHARE :])
 
@@ -236,22 +236,22 @@ def tile_list_expert_dispatch_down_kernel(
                     )
 
         z_turned = {
-            (b, part): keep.tile([P, T2 * K_PASS // P // parts], BF16, name=f"z_turned{b}_{part}")
-            for b, parts in enumerate(Z_PARTS)
-            for part in range(parts)
+            (b, part): keep.tile([P, T2 * K_PASS // P // 2], BF16, name=f"z_turned{b}_{part}")
+            for b in range(PASSES)
+            for part in range(2)
         }
         z_grouped, z_codes, z_plane = {}, {}, {}
 
-        def round_z(i, part, sums, copy):
+        def round_z(i, part, sums, copy, blocks=slice(0, 4)):
             b, quad = divmod(i, TILES_PER_PASS)
             rows = z_turned[b, part][:].rearrange("t (c u p e) -> t c u p e", u=2, p=P, e=2)
             copy(
-                rows[:, :, :, QUADRANT * quad : QUADRANT * (quad + 1), :],
+                rows[:, blocks, :, QUADRANT * quad : QUADRANT * (quad + 1), :],
                 sums.rearrange("t (c p u e) -> t c u p e", p=QUADRANT, u=2, e=2),
             )
 
         def turn_back(b, q, bank, identity):
-            part, m = divmod(q, 4 // Z_PARTS[b])
+            part, m = divmod(q, 2)
             words = z_turned[b, part][:].bitcast(F32).rearrange("t (c u p) -> t c u p", p=P, u=2)
             for c in range(2):
                 for u in range(2):
@@ -325,11 +325,8 @@ def tile_list_expert_dispatch_down_kernel(
             sum_pair = pairs[i % 3]
             turn_into(sum_pair, base_rows[i], True)
             turn_into(sum_pair, pages[i % PAGES], False)
-            parts = Z_PARTS[i // TILES_PER_PASS]
-            width = T2 // parts
-            for part in range(parts):
-                first = width * part % BANK
-                round_z(i, part, sum_pair[width * part // BANK][:, first : first + width], on_scalar)
+            for part in range(2):
+                round_z(i, part, sum_pair[part][:], on_scalar)
 
         group_wu(WU_CHUNKS[0])
         quantise_wu(0)
@@ -372,7 +369,7 @@ def tile_list_expert_dispatch_down_kernel(
                 tag = f"wu_raw{i + 1}_{PASSES - 1}"
             first = half if i == 0 else 0
             hidden = keep.tile([P, S - first], F32, name=f"hidden{i}", tag=tag, align_bytes=64)
-            if i < FIRST_SHARED:
+            if i not in SHARED:
                 product = early_banks[3][:, :half] if i == 0 else pairs[i % 3][0][:]
                 nc.vector.tensor_tensor(hidden[:], product, gates[i][:, first:], MULT)
             else:
@@ -386,25 +383,24 @@ def tile_list_expert_dispatch_down_kernel(
                 codes = new_codes("z_codes0_0", QUARTER, "weight_codes")
                 quantise_z(0, 0, 1, codes, new_plane("z_plane0_0", QUARTER, f"aside{LAST}"))
             scatter(i, hidden[:], first, S)
-            if 1 <= i <= 4:
-                gate_ahead(i + 1)
+            if i == 1:
+                gate_ahead(2)
             if 1 <= i < LAST:
                 sum_and_round(i - 1)
+            if 1 <= i <= LAST - 2:
+                gate_ahead(i + 2)
             if i == 1:
                 group_wu(WU_CHUNKS[4])
             if i == 3:
                 group_wu(WU_CHUNKS[5])
             if i == 4:
-                gate_ahead(6)
                 for q in range(4):
                     bank = (spare_bank, pairs[0][1])[q % 2]
                     turn_back(0, q, bank, ident)
                     group_z(0, q, bank)
             if i == 6:
                 group_wd(1, 0, 2)
-                group_wd(1, 2, 3)
             if i == 5:
-                gate_ahead(LAST)
                 group_wd(0, 0, 2)
                 group_wd(0, 2, 4)
 
@@ -414,15 +410,13 @@ def tile_list_expert_dispatch_down_kernel(
 
         sum_pair, last_up_bank = pairs[(LAST - 1) % 3], pairs[LAST % 3][0]
         turn_into(sum_pair, base_rows[LAST - 1], True)
-        turn_into(late_banks, base_rows[LAST], True)
         turn_into(sum_pair, pages[(LAST - 1) % PAGES], False)
+        turn_into(late_banks, base_rows[LAST], True)
         warm_up(last_up_bank, (S, P, P, P))
-        group_wd(1, 3, 4, f"page{(LAST - 1) % PAGES}")
-        for q in range(4):
-            first = QUARTER * (q % 2)
-            round_z(LAST - 1, q, sum_pair[q // 2][:, first : first + QUARTER], on_scalar)
-            if q % 2 == 1:
-                warm_up(sum_pair[q // 2], (S,) if q == 1 else (S, S))
+        for part in range(2):
+            round_z(LAST - 1, part, sum_pair[part][:], on_scalar)
+            warm_up(sum_pair[part], (S,) * (part + 1))
+        group_wd(1, 2, 4, tags[(LAST - 1) % PAGES])
         late_ident = keep.tile([P, P], F32, name="late_ident", tag="wd_raw1", align_bytes=64)
         on_scalar(late_ident[:], ident[:])
         turn_into(late_banks, pages[LAST % PAGES], False, late_ident)
@@ -437,10 +431,9 @@ def tile_list_expert_dispatch_down_kernel(
         quantise_wd(0, 2, 4)
         down_pass(out_pairs[0], 0, 0)
         quantise_wd(1, 0, 2)
-        quantise_wd(1, 2, 3)
-        quantise_wd(1, 3, 4)
+        quantise_wd(1, 2, 4)
         for q in range(4):
-            round_z(LAST, q, late_banks[q][:, :QUARTER], on_scalar)
+            round_z(LAST, q // 2, late_banks[q][:, :QUARTER], on_scalar, slice(2 * (q % 2), 2 * (q % 2) + 2))
 
         def finish(q):
             for m in range(2):

@@ -32,7 +32,7 @@ PAGES = 3
 GATES = 3
 WU_CHUNKS = ((0,), (1,), (2,), (3,), (4, 5), (6, 7))
 SHARE = P
-SHARED = (2, 4, 6, 7)
+SHARED = (1, 2, 4, 6, 7)
 WG_CHUNKS = ((0, 2), (2, 4), (4, 8))
 Z_PARTS = (2, 4)
 
@@ -400,6 +400,7 @@ def tile_list_expert_dispatch_down_kernel(
                     group_z(0, q, bank)
             if i == 6:
                 group_wd(1, 0, 2)
+                group_wd(1, 2, 4, f"aside{LAST - 1}")
             if i == 5:
                 group_wd(0, 0, 2)
                 group_wd(0, 2, 4)
@@ -416,8 +417,7 @@ def tile_list_expert_dispatch_down_kernel(
         for part in range(2):
             round_z(LAST - 1, part, sum_pair[part][:], on_scalar)
             warm_up(sum_pair[part], (S,) * (part + 1))
-        group_wd(1, 2, 4, tags[(LAST - 1) % PAGES])
-        late_ident = keep.tile([P, P], F32, name="late_ident", tag="wd_raw1", align_bytes=64)
+        late_ident = keep.tile([P, P], F32, name="late_ident", tag=tags[(LAST - 1) % PAGES], align_bytes=64)
         on_scalar(late_ident[:], ident[:])
         turn_into(late_banks, pages[LAST % PAGES], False, late_ident)
         out_pairs = [[last_up_bank, gate_bank], sum_pair, late_banks[0:2], late_banks[2:4]]

@@ -307,7 +307,7 @@ def tile_list_expert_dispatch_down_kernel(
                     stop=(b == PASSES - 1 and n % 2 == 1),
                 )
 
-        emptied_by = ((on_vector, on_vector), (on_scalar, on_scalar), (on_vector, on_scalar), (on_vector, on_scalar))
+        emptied_by = ((on_scalar, on_scalar), (on_scalar, on_scalar), (on_vector, on_scalar), (on_vector, on_scalar))
 
         def store(pair, q, m):
             result = keep.tile([P, 2, QUARTER], F32, name=f"result{q}_{m}", tag=f"base{2 * q + m}")

@@ -445,15 +445,38 @@ def tile_list_expert_dispatch_down_kernel(
 
         for q in range(4):
             turn_back(1, q, late_banks[q], late_ident)
+        last_codes, last_plane = new_codes("z_codes1_2", 2 * QUARTER, "z_codes1_2"), new_plane("z_plane1_2", 2 * QUARTER, "z_plane1_2")
+
+        def finish_half(n):
+            first_pass = late(2 * N + QUARTER, 2 * N + 3 * QUARTER)
+            for b, (codes, plane) in enumerate((first_pass, (last_codes, last_plane))):
+                nc.tensor.matmul_mx(
+                    out=late_banks[n][:],
+                    lhsT=wd_codes[b, n].bitcast(FP8X4),
+                    lhsT_scale=wd_plane[b, n],
+                    rhs=codes.bitcast(FP8X4),
+                    rhs_scale=plane,
+                    start=(b == 0),
+                    stop=(b == PASSES - 1),
+                )
+            result = keep.tile([P, 2 * QUARTER], F32, name=f"result_half{n}", tag=f"base{4 + n}")
+            (on_vector, on_scalar)[n % 2](result[:], late_banks[n][:])
+            nc.sync.dma_start(out[P * n : P * (n + 1), 2 * QUARTER :], result[:])
+
         for q in range(4):
             group_z(1, q, late_banks[q], on_vector if q == 0 else on_scalar)
             if q == 0:
                 quantise_z(0, 1, 2, *late(2 * N, 2 * N + QUARTER))
                 down_pass(out_pairs[1], 0, 1, range(2))
-            codes = new_codes(f"z_codes1_{q}", QUARTER, f"z_codes1_{q}")
-            quantise_z(1, q, q + 1, codes, new_plane(f"z_plane1_{q}", QUARTER, f"z_plane1_{q}"))
+            if q < 2:
+                codes = new_codes(f"z_codes1_{q}", QUARTER, f"z_codes1_{q}")
+                quantise_z(1, q, q + 1, codes, new_plane(f"z_plane1_{q}", QUARTER, f"z_plane1_{q}"))
+            else:
+                cols = slice(QUARTER * (q - 2), QUARTER * (q - 1))
+                quantise_z(1, q, q + 1, last_codes[:, cols], last_plane[:, cols])
             if q == 1:
                 finish(0)
                 quantise_z(0, 2, 4, *late(2 * N + QUARTER, 2 * N + 3 * QUARTER))
-        for q in range(1, 4):
-            finish(q)
+        finish(1)
+        for n in range(N // P):
+            finish_half(n)

@@ -77,7 +77,7 @@ def tile_list_expert_dispatch_down_kernel(
                     wg_plane[i, a] = plane[:, col : col + P]
 
         tab_plane = keep.tile([P, PASSES * T], U8, name="tab_plane", tag="tab_plane", align_bytes=64)
-        nc.vector.memset(tab_plane[:].bitcast(I32), 0)
+        nc.gpsimd.memset(tab_plane[:].bitcast(I32), 0)
 
         table = [keep.tile([P, T], I32, name=f"table{a}", align_bytes=64) for a in range(PASSES)]
         wu_raw, wg_codes, base_rows, wd_raw = {}, {}, {}, {}
@@ -115,8 +115,8 @@ def tile_list_expert_dispatch_down_kernel(
             tab_scales.bitcast(I32).rearrange("a q c -> q a c"),
         )
         load_wu(WU_CHUNKS[0], [1])
-        load_table(0)
         load_wg(*WG_CHUNKS[0])
+        load_table(0)
         load_wg_plane(*WG_CHUNKS[0])
         load_table(1)
 

@@ -438,8 +438,6 @@ def tile_list_expert_dispatch_down_kernel(
         def finish(q):
             for m in range(2):
                 row_tiles = range(2 * m, 2 * m + 2)
-                if 2 * q + m >= 3:
-                    down_pass(out_pairs[q], 0, q, row_tiles)
                 down_pass(out_pairs[q], 1, q, row_tiles)
                 store(out_pairs[q], q, m)
 
@@ -467,7 +465,7 @@ def tile_list_expert_dispatch_down_kernel(
             group_z(1, q, late_banks[q], on_vector if q == 0 else on_scalar)
             if q == 0:
                 quantise_z(0, 1, 2, *late(2 * N, 2 * N + QUARTER))
-                down_pass(out_pairs[1], 0, 1, range(2))
+                down_pass(out_pairs[1], 0, 1)
             if q < 2:
                 codes = new_codes(f"z_codes1_{q}", QUARTER, f"z_codes1_{q}")
                 quantise_z(1, q, q + 1, codes, new_plane(f"z_plane1_{q}", QUARTER, f"z_plane1_{q}"))

@@ -31,7 +31,7 @@ QUARTER = T2 // 4
 PAGES = 3
 GATES = 3
 WU_CHUNKS = ((0,), (1,), (2,), (3,), (4, 5), (6, 7))
-SHARE = P
+SHARE = 96
 SHARED = (1, 2, 4, 6, 7)
 WG_CHUNKS = ((0, 2), (2, 4), (4, 8))
 Z_PARTS = (2, 4)

from contextlib import ExitStack

import concourse.mybir as mybir
from concourse.masks import make_identity

K, T, S, H, T2, N = 1024, 2048, 512, 1024, 1024, 512
FLOPS = 2 * (2 * K * H * S + H * N * T2)

F32 = mybir.dt.float32
BF16 = mybir.dt.bfloat16
I32 = mybir.dt.int32
U32 = mybir.dt.uint32
U16 = mybir.dt.uint16
U8 = mybir.dt.uint8
FP8X4 = mybir.dt.float8_e4m3fn_x4
FP4X4 = mybir.dt.float4_e2m1fn_x4
MULT = mybir.AluOpType.mult
SILU = mybir.ActivationFunctionType.Silu

P = 128
SLOTS = 4
K_PASS = P * SLOTS
PASSES = 2
QUADRANT = 32
SPREAD = 8
BANK = 512
ROW_TILES = H // P
LAST = ROW_TILES - 1
TILES_PER_PASS = K_PASS // P
QUARTER = T2 // 4
PAGES = 3
GATES = 3
WU_CHUNKS = ((0,), (1,), (2,), (3,), (4, 5), (6, 7))
SHARE = 96
SHARED = (1, 2, 4, 6, 7)
WG_CHUNKS = ((0, 2), (2, 4), (4, 8))
Z_PARTS = (2, 4)


def tile_list_expert_dispatch_down_kernel(
    tc, tab_words, tab_scales, offs, wu, wg_words, wg_scales, offs2, wgs, base, wd, out
):
    nc = tc.nc
    on_scalar, on_vector = nc.scalar.copy, nc.vector.tensor_copy
    with ExitStack() as ctx:
        lists = ctx.enter_context(tc.tile_pool(name="lists", bufs=1))
        keep = ctx.enter_context(tc.tile_pool(name="keep", bufs=1))
        psum = ctx.enter_context(tc.psum_pool(name="psum", bufs=1))

        banks = [psum.tile([P, BANK], F32, name=f"bank{b}") for b in range(8)]
        pairs, gate_bank, spare_bank = (banks[0:2], banks[2:4], banks[4:6]), banks[6], banks[7]
        early_banks = pairs[2] + pairs[0]
        late_banks = [pairs[1][1], spare_bank] + pairs[2]

        idx = lists.tile([P, S // 16], U16, name="idx")
        idx2 = lists.tile([P, S // 16], U16, name="idx2")
        nc.sync.dma_start(idx[:], offs)
        nc.sync.dma_start(idx2[:], offs2)

        def load_plane(plane, scales):
            for r in range(4):
                live = plane[r:P:QUADRANT, :]
                nc.sync.dma_start(
                    live.bitcast(I32).rearrange("q (a c) -> q a c", a=PASSES),
                    scales[:, r:16:4, :].bitcast(I32).rearrange("a q c -> q a c"),
                )

        wg_plane = {}

        def load_wg_plane(first, end):
            width = P * (end - first)
            plane = keep.tile([P, PASSES * width], U8, name=f"wg_plane{first}", align_bytes=64)
            load_plane(plane, wg_scales[:, :, P * first : P * end])
            for i in range(first, end):
                for a in range(PASSES):
                    col = width * a + P * (i - first)
                    wg_plane[i, a] = plane[:, col : col + P]

        tab_plane = keep.tile([P, PASSES * T], U8, name="tab_plane", tag="tab_plane", align_bytes=64)
        nc.gpsimd.memset(tab_plane[:].bitcast(I32), 0)

        table = [keep.tile([P, T], I32, name=f"table{a}", align_bytes=64) for a in range(PASSES)]
        wu_raw, wg_codes, base_rows, wd_raw = {}, {}, {}, {}

        def load_wu(chunk, passes=range(PASSES)):
            width = P * len(chunk)
            for a in passes:
                tag = f"wu_raw{chunk[0]}_{a}"
                wu_raw[chunk, a] = keep.tile([P, SLOTS, width], F32, name=tag, tag=tag, align_bytes=64)
                rows = wu[K_PASS * a : K_PASS * (a + 1), P * chunk[0] : P * chunk[0] + width]
                nc.sync.dma_start(wu_raw[chunk, a][:], rows.rearrange("(p j) c -> p j c", j=SLOTS))

        def load_wg(first, end):
            cols = slice(2 * P * first, 2 * P * end)
            words = keep.tile([P, PASSES, 2 * P * (end - first)], U8, name=f"wg_words{first}", align_bytes=64)
            nc.sync.dma_start(words[:].bitcast(I32), wg_words[:, :, cols].bitcast(I32).rearrange("a p c -> p a c"))
            for i in range(first, end):
                wg_codes[i] = words[:, :, 2 * P * (i - first) : 2 * P * (i - first + 1)]

        def load_base(i):
            base_rows[i] = keep.tile([P, T2], F32, name=f"base{i}", tag=f"base{i}")
            nc.sync.dma_start(base_rows[i][:], base[P * i : P * (i + 1), :])

        def load_wd(b):
            wd_raw[b] = keep.tile([P, SLOTS, N], F32, name=f"wd_raw{b}", tag=f"wd_raw{b}", align_bytes=64)
            rows = wd[K_PASS * b : K_PASS * (b + 1), :]
            nc.sync.dma_start(wd_raw[b][:], rows.rearrange("(p j) n -> p j n", j=SLOTS))

        def load_table(a):
            nc.sync.dma_start(table[a][:], tab_words[a].rearrange("p t i -> p (t i)").bitcast(I32))

        load_wu(WU_CHUNKS[0], [0])
        nc.sync.dma_start(
            tab_plane[0:P:SPREAD, :].bitcast(I32).rearrange("q (a c) -> q a c", a=PASSES),
            tab_scales.bitcast(I32).rearrange("a q c -> q a c"),
        )
        load_wu(WU_CHUNKS[0], [1])
        load_wg(*WG_CHUNKS[0])
        load_table(0)
        load_wg_plane(*WG_CHUNKS[0])
        load_table(1)

        ident = keep.tile([P, P], F32, name="ident", tag="ident", align_bytes=64)
        nc.vector.memset(ident[:], 0.0)
        make_identity(nc, ident[:], nomemset=True)
        picked = keep.tile([P, PASSES * S], U8, name="picked", align_bytes=64)
        moved = keep.tile([P, PASSES * S], U8, name="moved", align_bytes=64)
        v_plane = [moved[:, S * a : S * (a + 1)] for a in range(PASSES)]
        v_codes = [keep.tile([P, S], U32, name=f"v_codes{a}", align_bytes=64) for a in range(PASSES)]
        for a in range(PASSES):
            nc.vector.tensor_copy(picked[:, S * a : S * (a + 1)], tab_plane[:, T * a : T * (a + 1)].indirect(idx[:]))
        for r in range(4):
            nc.sync.dma_start(moved[r:P:QUADRANT, :].bitcast(I32), picked[SPREAD * r : P : QUADRANT, :].bitcast(I32))
        nc.vector.tensor_copy(v_codes[0][:], table[0][:].bitcast(U32).indirect(idx[:]))
        load_wu(WU_CHUNKS[1])
        weights = keep.tile([P, S], F32, name="weights")
        nc.sync.dma_start(weights[:], wgs)
        load_wu(WU_CHUNKS[2])
        load_wu(WU_CHUNKS[3])
        load_wg(*WG_CHUNKS[1])
        load_wg_plane(WG_CHUNKS[1][0], ROW_TILES)
        load_wu(WU_CHUNKS[4])
        load_base(0)
        load_base(1)
        load_wg(*WG_CHUNKS[2])
        load_base(2)
        load_wu(WU_CHUNKS[5])
        load_base(3)
        load_wd(0)
        load_base(4)
        load_wd(1)
        for i in (LAST, 5, 6):
            load_base(i)


        tags = [f"page{n}" for n in range(PAGES - 1)] + ["tab_plane"]
        pages = [keep.tile([P, T2], F32, name=f"page{n}", tag=tags[n], align_bytes=64) for n in range(PAGES)]
        for page in pages:
            nc.vector.memset(page[:], 0.0)

        wu_codes, wu_plane, gates = {}, {}, {}

        wu_grouped = {}

        def group_wu(chunk):
            tiles = len(chunk)
            grouped = keep.tile([P, tiles * PASSES * K_PASS], BF16, name=f"wu_grouped{chunk[0]}", align_bytes=64)
            target = grouped[:].rearrange("p (n a c w j) -> p a n c j w", n=tiles, a=PASSES, w=4, j=SLOTS)
            for a in range(PASSES):
                on_scalar(target[:, a], wu_raw[chunk, a][:].rearrange("p j (n c w) -> p n c j w", n=tiles, w=4))
            for n, i in enumerate(chunk):
                wu_grouped[i] = grouped[:, PASSES * K_PASS * n : PASSES * K_PASS * (n + 1)]

        def quantise_wu(i):
            codes = keep.tile([P, PASSES * P], U32, name=f"wu_codes{i}", tag="weight_codes", align_bytes=64)
            plane = keep.tile([P, PASSES * P], U8, name=f"wu_plane{i}", tag=f"aside{i - 1}", align_bytes=64)
            nc.vector.quantize_mx(out=codes[:].bitcast(FP8X4), scales=plane[:], in_=wu_grouped[i])
            for a in range(PASSES):
                cols = slice(P * a, P * (a + 1))
                wu_codes[i, a], wu_plane[i, a] = codes[:, cols], plane[:, cols]

        def gate_pass(i, a, target, entries, start, stop):
            nc.tensor.matmul_mx(
                out=target,
                lhsT=wg_codes[i][:, a, :].bitcast(FP4X4),
                lhsT_scale=wg_plane[i, a],
                rhs=v_codes[a][:, entries].bitcast(FP8X4),
                rhs_scale=v_plane[a][:, entries],
                start=start,
                stop=stop,
            )

        def up_pass(i, a, target, entries):
            nc.tensor.matmul_mx(
                out=target,
                lhsT=wu_codes[i, a].bitcast(FP8X4),
                lhsT_scale=wu_plane[i, a],
                rhs=v_codes[a][:, entries].bitcast(FP8X4),
                rhs_scale=v_plane[a][:, entries],
                start=(a == 0),
                stop=(a == PASSES - 1),
            )

        def gate_product(i):
            for a in range(PASSES):
                gate_pass(i, a, gate_bank[:], slice(0, S), a == 0, a == PASSES - 1)

        aside = {}

        def up_product(i):
            for a in range(PASSES):
                up_pass(i, a, pairs[i % 3][0][:], slice(0, S))
            if i in SHARED:
                aside[i] = keep.tile([P, SHARE], F32, name=f"aside{i}", tag=f"aside{i}", align_bytes=64)
                on_scalar(aside[i][:], pairs[i % 3][0][:, S - SHARE :])

        def new_gate(i):
            gates[i] = keep.tile([P, S], F32, name=f"gate{i}", tag=f"gate{i % GATES}", align_bytes=64)

        def activate(i):
            new_gate(i)
            nc.scalar.activation(gates[i][:], gate_bank[:], SILU)

        def turn_into(group, rows, opens, identity=ident):
            blocks = T2 // P // len(group)
            for place, bank in enumerate(group):
                for c in range(blocks):
                    t0 = P * (blocks * place + c)
                    nc.tensor.matmul(
                        bank[:, P * c : P * (c + 1)],
                        lhsT=rows[:, t0 : t0 + P],
                        rhs=identity[:],
                        is_transpose=True,
                        start=(opens and c == 0),
                        stop=(not opens and c == blocks - 1),
                    )

        z_turned = {
            (b, part): keep.tile([P, T2 * K_PASS // P // 2], BF16, name=f"z_turned{b}_{part}")
            for b in range(PASSES)
            for part in range(2)
        }
        z_grouped, z_codes, z_plane = {}, {}, {}

        def round_z(i, part, sums, copy, blocks=slice(0, 4)):
            b, quad = divmod(i, TILES_PER_PASS)
            rows = z_turned[b, part][:].rearrange("t (c u p e) -> t c u p e", u=2, p=P, e=2)
            copy(
                rows[:, blocks, :, QUADRANT * quad : QUADRANT * (quad + 1), :],
                sums.rearrange("t (c p u e) -> t c u p e", p=QUADRANT, u=2, e=2),
            )

        def turn_back(b, q, bank, identity):
            part, m = divmod(q, 2)
            words = z_turned[b, part][:].bitcast(F32).rearrange("t (c u p) -> t c u p", p=P, u=2)
            for c in range(2):
                for u in range(2):
                    col = P * (2 * c + u)
                    nc.tensor.transpose(bank[:, col : col + P], words[:, 2 * m + c, u, :], identity[:])

        def group_z(b, q, bank, copy=on_scalar):
            part, m = divmod(q, 4 // Z_PARTS[b])
            if m == 0:
                width = 2 * T2 // Z_PARTS[b]
                z_grouped[b, part] = keep.tile([P, width], F32, name=f"z_grouped{b}_{part}", align_bytes=64)
            target = z_grouped[b, part][:, 2 * QUARTER * m : 2 * QUARTER * (m + 1)]
            copy(
                target.rearrange("p (c t u) -> p c t u", c=2, u=2),
                bank[:].rearrange("p (c u t) -> p c t u", c=2, u=2),
            )

        def quantise_z(b, first, end, codes, plane):
            part, m = divmod(first, 4 // Z_PARTS[b])
            words = z_grouped[b, part][:, 2 * QUARTER * m : 2 * QUARTER * (m + end - first)]
            nc.vector.quantize_mx(out=codes.bitcast(FP8X4), scales=plane, in_=words.bitcast(BF16))
            for q in range(first, end):
                cols = slice(QUARTER * (q - first), QUARTER * (q - first + 1))
                z_codes[b, q], z_plane[b, q] = codes[:, cols], plane[:, cols]

        wd_grouped, wd_codes, wd_plane = {}, {}, {}

        def group_wd(b, first, end, tag=None):
            name = f"wd_grouped{b}_{first}"
            width = K_PASS * (end - first)
            wd_grouped[b, first] = keep.tile([P, width], BF16, name=name, tag=tag or name, align_bytes=64)
            target = wd_grouped[b, first][:].rearrange("p (c w j) -> p c j w", w=4, j=SLOTS)
            source = wd_raw[b][:, :, P * first : P * end].rearrange("p j (c w) -> p c j w", w=4)
            on_scalar(target, source)

        def quantise_wd(b, first, end):
            place = N * b + P * first
            codes, plane = late(place, place + P * (end - first))
            nc.vector.quantize_mx(out=codes.bitcast(FP8X4), scales=plane, in_=wd_grouped[b, first][:])
            for n in range(first, end):
                cols = slice(P * (n - first), P * (n - first + 1))
                wd_codes[b, n], wd_plane[b, n] = codes[:, cols], plane[:, cols]

        def down_pass(pair, b, q, row_tiles=range(N // P)):
            for n in row_tiles:
                nc.tensor.matmul_mx(
                    out=pair[n // 2][:, QUARTER * (n % 2) : QUARTER * (n % 2 + 1)],
                    lhsT=wd_codes[b, n].bitcast(FP8X4),
                    lhsT_scale=wd_plane[b, n],
                    rhs=z_codes[b, q].bitcast(FP8X4),
                    rhs_scale=z_plane[b, q],
                    start=(b == 0 and n % 2 == 0),
                    stop=(b == PASSES - 1 and n % 2 == 1),
                )

        emptied_by = ((on_scalar, on_scalar), (on_scalar, on_scalar), (on_vector, on_scalar), (on_vector, on_scalar))

        def store(pair, q, m):
            result = keep.tile([P, 2, QUARTER], F32, name=f"result{q}_{m}", tag=f"base{2 * q + m}")
            emptied_by[q][m](result[:].rearrange("p n t -> p (n t)"), pair[m][:])
            rows = out[2 * P * m : 2 * P * (m + 1), QUARTER * q : QUARTER * (q + 1)]
            nc.sync.dma_start(rows.rearrange("(n p) t -> p n t", n=2), result[:])

        def new_codes(name, width, tag):
            return keep.tile([P, width], U32, name=name, tag=tag, align_bytes=64)[:]

        def new_plane(name, width, tag):
            return keep.tile([P, width], U8, name=name, tag=tag, align_bytes=64)[:]

        def sum_and_round(i):
            sum_pair = pairs[i % 3]
            turn_into(sum_pair, base_rows[i], True)
            turn_into(sum_pair, pages[i % PAGES], False)
            for part in range(2):
                round_z(i, part, sum_pair[part][:], on_scalar)

        group_wu(WU_CHUNKS[0])
        quantise_wu(0)
        half = S // 2
        halves = [slice(half * n, half * (n + 1)) for n in range(2)]
        new_gate(0)
        for n, entries in enumerate(halves):
            places = idx[:, entries.start // 16 : entries.stop // 16]
            nc.vector.tensor_copy(v_codes[1][:, entries], table[1][:].bitcast(U32).indirect(places))
            for a in range(PASSES):
                gate_pass(0, a, early_banks[n][:, :half], entries, a == 0, a == PASSES - 1)
            nc.scalar.activation(gates[0][:, entries], early_banks[n][:, :half], SILU)
            if n == 0:
                group_wu(WU_CHUNKS[1])
            for a in range(PASSES):
                up_pass(0, a, early_banks[2 + n][:, :half], entries)
        gate_product(1)

        def scatter(i, hidden, first, end):
            places = idx2[:, first // 16 : end // 16]
            nc.vector.tensor_tensor(pages[i % PAGES][:].indirect(places), hidden, weights[:, first:end], MULT)

        early = keep.tile([P, half], F32, name="hidden_early")
        nc.vector.tensor_tensor(early[:], early_banks[2][:, :half], gates[0][:, :half], MULT)
        scatter(0, early[:], 0, half)

        def gate_ahead(i):
            activate(i)
            if i < LAST:
                gate_product(i + 1)

        for i in range(ROW_TILES):
            tag = f"hidden{i}"
            if i <= 1:
                if i == 1:
                    gate_ahead(1)
                    group_wu(WU_CHUNKS[2])
                    group_wu(WU_CHUNKS[3])
            if i in (0, 1, 2, 3, 5):
                tag = f"wu_raw{i + 1}_{PASSES - 1}"
            first = half if i == 0 else 0
            hidden = keep.tile([P, S - first], F32, name=f"hidden{i}", tag=tag, align_bytes=64)
            if i not in SHARED:
                product = early_banks[3][:, :half] if i == 0 else pairs[i % 3][0][:]
                nc.vector.tensor_tensor(hidden[:], product, gates[i][:, first:], MULT)
            else:
                cut = S - SHARE
                nc.vector.tensor_tensor(hidden[:, :cut], pairs[i % 3][0][:, :cut], gates[i][:, :cut], MULT)
                nc.gpsimd.tensor_tensor(hidden[:, cut:], aside[i][:], gates[i][:, cut:], MULT)
            if i < LAST:
                quantise_wu(i + 1)
                up_product(i + 1)
            else:
                codes = new_codes("z_codes0_0", QUARTER, "weight_codes")
                quantise_z(0, 0, 1, codes, new_plane("z_plane0_0", QUARTER, f"aside{LAST}"))
            scatter(i, hidden[:], first, S)
            if i == 1:
                gate_ahead(2)
            if 1 <= i < LAST:
                sum_and_round(i - 1)
            if 1 <= i <= LAST - 2:
                gate_ahead(i + 2)
            if i == 1:
                group_wu(WU_CHUNKS[4])
            if i == 3:
                group_wu(WU_CHUNKS[5])
            if i == 4:
                for q in range(4):
                    bank = (spare_bank, pairs[0][1])[q % 2]
                    turn_back(0, q, bank, ident)
                    group_z(0, q, bank)
            if i == 6:
                group_wd(1, 0, 2)
                group_wd(1, 2, 4, f"aside{LAST - 1}")
            if i == 5:
                group_wd(0, 0, 2)
                group_wd(0, 2, 4)

        def warm_up(bank, widths):
            for n, width in enumerate(widths):
                gate_pass(LAST, 0, bank[:, :width], slice(0, width), n == 0, n == len(widths) - 1)

        sum_pair, last_up_bank = pairs[(LAST - 1) % 3], pairs[LAST % 3][0]
        turn_into(sum_pair, base_rows[LAST - 1], True)
        turn_into(sum_pair, pages[(LAST - 1) % PAGES], False)
        turn_into(late_banks, base_rows[LAST], True)
        warm_up(last_up_bank, (S, P, P, P))
        for part in range(2):
            round_z(LAST - 1, part, sum_pair[part][:], on_scalar)
            warm_up(sum_pair[part], (S,) * (part + 1))
        late_ident = keep.tile([P, P], F32, name="late_ident", tag=tags[(LAST - 1) % PAGES], align_bytes=64)
        on_scalar(late_ident[:], ident[:])
        turn_into(late_banks, pages[LAST % PAGES], False, late_ident)
        out_pairs = [[last_up_bank, gate_bank], sum_pair, late_banks[0:2], late_banks[2:4]]
        late_planes = new_plane("late_planes", 7 * QUARTER, f"hidden{LAST}")
        late_codes = new_codes("late_codes", 7 * QUARTER, "ident")

        def late(first, end):
            return late_codes[:, first:end], late_planes[:, first:end]

        quantise_wd(0, 0, 2)
        quantise_wd(0, 2, 4)
        down_pass(out_pairs[0], 0, 0)
        quantise_wd(1, 0, 2)
        quantise_wd(1, 2, 4)
        for q in range(4):
            round_z(LAST, q // 2, late_banks[q][:, :QUARTER], on_scalar, slice(2 * (q % 2), 2 * (q % 2) + 2))

        def finish(q):
            for m in range(2):
                row_tiles = range(2 * m, 2 * m + 2)
                down_pass(out_pairs[q], 1, q, row_tiles)
                store(out_pairs[q], q, m)

        for q in range(4):
            turn_back(1, q, late_banks[q], late_ident)
        last_codes, last_plane = new_codes("z_codes1_2", 2 * QUARTER, "z_codes1_2"), new_plane("z_plane1_2", 2 * QUARTER, "z_plane1_2")

        def finish_half(n):
            first_pass = late(2 * N + QUARTER, 2 * N + 3 * QUARTER)
            for b, (codes, plane) in enumerate((first_pass, (last_codes, last_plane))):
                nc.tensor.matmul_mx(
                    out=late_banks[n][:],
                    lhsT=wd_codes[b, n].bitcast(FP8X4),
                    lhsT_scale=wd_plane[b, n],
                    rhs=codes.bitcast(FP8X4),
                    rhs_scale=plane,
                    start=(b == 0),
                    stop=(b == PASSES - 1),
                )
            result = keep.tile([P, 2 * QUARTER], F32, name=f"result_half{n}", tag=f"base{4 + n}")
            (on_vector, on_scalar)[n % 2](result[:], late_banks[n][:])
            nc.sync.dma_start(out[P * n : P * (n + 1), 2 * QUARTER :], result[:])

        for q in range(4):
            group_z(1, q, late_banks[q], on_vector if q == 0 else on_scalar)
            if q == 0:
                quantise_z(0, 1, 2, *late(2 * N, 2 * N + QUARTER))
                down_pass(out_pairs[1], 0, 1)
            if q < 2:
                codes = new_codes(f"z_codes1_{q}", QUARTER, f"z_codes1_{q}")
                quantise_z(1, q, q + 1, codes, new_plane(f"z_plane1_{q}", QUARTER, f"z_plane1_{q}"))
            else:
                cols = slice(QUARTER * (q - 2), QUARTER * (q - 1))
                quantise_z(1, q, q + 1, last_codes[:, cols], last_plane[:, cols])
            if q == 1:
                finish(0)
                quantise_z(0, 2, 4, *late(2 * N + QUARTER, 2 * N + 3 * QUARTER))
        finish(1)
        for n in range(N // P):
            finish_half(n)
